import numpy as np
import ml_dtypes


def mxq(x, axis, fmt="e4m3"):
    dtype, down = {"e4m3": (ml_dtypes.float8_e4m3fn, 7), "e5m2": (ml_dtypes.float8_e5m2, 14)}[fmt]
    v = np.moveaxis(np.asarray(x, np.float32).astype(ml_dtypes.bfloat16).astype(np.float64), axis, -1)
    blocks = v.reshape(v.shape[:-1] + (-1, 32))
    amax = np.abs(blocks).max(-1, keepdims=True)
    byte = np.maximum(np.where(amax > 0, np.frexp(amax)[1] - 1 + 127, 0) - down, 1)
    scale = np.exp2(byte - 127.0)
    codes = (blocks / scale).astype(np.float32).astype(dtype).astype(np.float64)
    return np.moveaxis((codes * scale).reshape(v.shape), -1, axis)


WIDE = False


def mx_kscale(k):
    if not WIDE:
        return np.ones(k)
    levels = np.array([10, -10, 5, -5, 0])
    if k % 512:
        return np.exp2(np.random.permutation(np.resize(levels, k // 32))).repeat(32)
    a = np.empty((k // 512, 16))
    for p in range(k // 512):
        a[p, :8] = np.random.permutation(np.resize(levels, 8))
        for g in range(8):
            far = levels[np.abs(levels - a[p, g]) >= 10]
            a[p, g + 8] = far[np.random.randint(len(far))]
    return np.exp2(a.ravel()).repeat(32)


def f64(x):
    return np.asarray(x).astype(np.float64)


def striped(idx):
    return np.tile(idx.reshape(-1, 16).T, (8, 1)).astype(np.uint16)


def unstriped(offs):
    return offs[:16].T.reshape(-1).astype(np.int64)


E2M1 = np.array([0.0, 0.5, 1.0, 1.5, 2.0, 3.0, 4.0, 6.0, -0.0, -0.5, -1.0, -1.5, -2.0, -3.0, -4.0, -6.0])


def pack_weight(w, fmt):
    k, n = w.shape
    w = f64(np.asarray(w, np.float32).astype(ml_dtypes.bfloat16)).reshape(k // 32, 32, n)
    amax = np.abs(w).max(1)
    if fmt == "e4m3":
        byte = np.frexp(amax)[1] - 1 + 127 - 7
    else:
        mant, ex = np.frexp(amax / 6.0)
        byte = np.where(mant > 0.5, ex, ex - 1) + 127
    byte = np.clip(np.where(amax > 0, byte, 1), 1, 254)
    scaled = (w * np.exp2(127.0 - byte)[:, None, :]).reshape(k, n).astype(np.float32)
    by_word = np.ascontiguousarray(scaled.reshape(k // 512, 128, 4, n).transpose(0, 1, 3, 2))
    if fmt == "e4m3":
        words = by_word.astype(ml_dtypes.float8_e4m3fn).view(np.uint8)
    else:
        c = by_word.astype(ml_dtypes.float4_e2m1fn).view(np.uint8) & 0xF
        words = (c[..., 0::2] | (c[..., 1::2] << 4)).reshape(k // 512, 128, 2 * n)
    return np.ascontiguousarray(words), np.ascontiguousarray(byte.astype(np.uint8).reshape(k // 512, 16, n))


def unpack_weight(words, scales, fmt):
    g, _, n = scales.shape
    words = np.ascontiguousarray(words).reshape(g, 128, n, -1)
    if fmt == "e4m3":
        vals = words.view(ml_dtypes.float8_e4m3fn).astype(np.float64)
    else:
        nib = np.empty((g, 128, n, 4), np.uint8)
        nib[..., 0::2] = words & 0xF
        nib[..., 1::2] = words >> 4
        vals = E2M1[nib]
    vals = vals * np.repeat(np.exp2(scales.astype(np.float64) - 127.0), 8, axis=1)[..., None]
    return vals.transpose(0, 1, 3, 2).reshape(g * 512, n)


def gelu(v):
    return 0.5 * v * (1.0 + np.tanh(np.sqrt(2.0 / np.pi) * (v + 0.044715 * v**3)))


K, T, S, H, T2, P, N = 1024, 4096, 1024, 1024, 2048, 1024, 512

def setup_inputs():
    n = np.random.standard_normal
    s = mx_kscale(K)[:, None]
    u = mx_kscale(H)[:, None]
    tab_words, tab_scales = pack_weight(n((K, T)) * s, "e4m3")
    w1 = (n((K, H)) / np.sqrt(K) / s * u.T).astype(np.float32)
    wb_words, wb_scales = pack_weight(n((H, N)) / np.sqrt(H) / u, "e2m1")
    wp = (n((H, N)) / np.sqrt(H) / u).astype(np.float32)
    page0 = (n((H, T2)) * u).astype(np.float32)
    wgs = np.exp(0.3 * n((128, S))).astype(np.float32)
    return {"tab_words": tab_words, "tab_scales": tab_scales,
            "offs": striped(np.random.permutation(T)[:S]),
            "offs2": striped(np.random.permutation(T2)[:S]),
            "offs3": striped(np.random.permutation(T2)[:P]),
            "w1": w1, "wgs": wgs, "page0": page0,
            "wb_words": wb_words, "wb_scales": wb_scales, "wp": wp}

def reference(tab_words, tab_scales, offs, offs2, offs3, w1, wgs, page0, wb_words, wb_scales, wp):
    v = unpack_weight(tab_words, tab_scales, "e4m3")[:, unstriped(offs)]
    h = mxq(f64(w1), 0, "e4m3").T @ v
    page = f64(page0).copy()
    page[:, unstriped(offs2)] = np.tile(f64(wgs), (H // 128, 1)) * h
    x = page[:, unstriped(offs3)]
    z = mxq(np.maximum(x, 0.0), 0, "e4m3")
    brand = unpack_weight(wb_words, wb_scales, "e2m1").T @ z
    perf = mxq(f64(wp), 0, "e4m3").T @ z
    return np.maximum(brand, perf)

@@ -1,0 +1,324 @@
+from contextlib import ExitStack
+
+import concourse.mybir as mybir
+
+K, T, S, H, T2, SLOTS, N = 1024, 4096, 1024, 1024, 2048, 1024, 512
+FLOPS = 2 * K * H * S + 2 * 2 * H * N * SLOTS
+
+F32 = mybir.dt.float32
+BF16 = mybir.dt.bfloat16
+I32 = mybir.dt.int32
+U32 = mybir.dt.uint32
+U16 = mybir.dt.uint16
+U8 = mybir.dt.uint8
+FP8X4 = mybir.dt.float8_e4m3fn_x4
+FP4X4 = mybir.dt.float4_e2m1fn_x4
+MULT = mybir.AluOpType.mult
+MAX = mybir.AluOpType.max
+RELU = mybir.ActivationFunctionType.Relu
+
+P = 128
+PACK = 4
+K_PASS = P * PACK
+BANK = 512
+CHUNK = 256
+QUADS = 4
+
+
+KB = 1024
+
+
+def tile_list_slot_bidding_kernel(
+    tc, tab_words, tab_scales, offs, offs2, offs3, w1, wgs, page0, wb_words, wb_scales, wp, out
+):
+    nc = tc.nc
+    with ExitStack() as ctx:
+        lists = ctx.enter_context(tc.tile_pool(name="lists", bufs=1))
+        keep = ctx.enter_context(tc.tile_pool(name="keep", bufs=1))
+        shared = ctx.enter_context(tc.tile_pool(name="shared", bufs=1))
+        psum = ctx.enter_context(tc.psum_pool(name="psum", bufs=1))
+        banks = [psum.tile([P, BANK], F32, name=f"bank{b}") for b in range(8)]
+
+        def own(name, shape, dtype):
+            return keep.tile(shape, dtype, name=name, align_bytes=64)
+
+        def placed(name, shape, dtype, kb):
+            return shared.tile(shape, dtype, name=name, align_bytes=64, offset=kb * KB)
+
+        TAB, TAB_SC, PAGES, W1_FIRST, W1_REST, W1_UPPER, WGS_PLANES = 0, 32, 36, 84, 88, 100, 116
+        G_FIRST, G_REST1, G_REST2, G_UPPER, H0B, H1, X_ROWS2, ZG_HIGH, G_WP = 132, 134, 136, 140, 148, 150, 170, 174, 182
+        H7 = W1_REST + 4
+
+        list1 = lists.tile([P, S // 16], U16, name="list1")
+        list2 = lists.tile([P, S // 16], U16, name="list2")
+        list3 = lists.tile([P, SLOTS // 16], U16, name="list3")
+        tab = [placed(f"tab{a}", [P, T], I32, TAB + 16 * a) for a in range(2)]
+        tab_sc = placed("tab_sc", [P, T], U8, TAB_SC)
+        v_sc = own("v_sc", [P, S], U8)
+        wb_codes = own("wb_codes", [P, 2, 2 * N], U8)
+        wb_sc = own("wb_sc", [P, 2, N], U8)
+        wgs_rows = own("wgs_rows", [P, S], F32)
+
+        def pass_rows(w, a):
+            return w[a * K_PASS : (a + 1) * K_PASS, :].rearrange("(p j) c -> p j c", j=PACK)
+
+        pages = {}
+
+        def load_page(index):
+            pages[index] = placed(f"page{index}", [P, T2], F32, PAGES + 8 * (index % 6))
+            if index < 4:
+                rows = page0[index * P : (index + 1) * P, :]
+            else:
+                rows = page0[K_PASS:, :].rearrange("(p i) t -> i p t", i=PACK)[index - 4]
+            nc.sync.dma_start(out=pages[index][:], in_=rows)
+
+        def load(name, rows, kb):
+            raw = placed(name, list(rows.shape), F32, kb)
+            nc.sync.dma_start(out=raw[:], in_=rows)
+            return raw
+
+        def quantize(name, grouped, width, kb=None):
+            shape = [P, width // PACK]
+            codes = own(name + "_codes", shape, U32) if kb is None else placed(name + "_codes", shape, U32, kb)
+            scales = own(name + "_sc", shape, U8)
+            nc.vector.quantize_mx(out=codes[:].bitcast(FP8X4), scales=scales[:], in_=grouped)
+            return codes, scales
+
+        def woven(flat):
+            return flat.rearrange("p (c i j) -> p c j i", i=4, j=PACK)
+
+        def planar(planes):
+            return planes.rearrange("p j (c i) -> p c j i", i=4)
+
+        nc.vector.memset(tab_sc[:].bitcast(I32), 0)
+        nc.vector.memset(wb_sc[:].rearrange("p a c -> p (a c)").bitcast(I32), 0)
+        for q in range(QUADS):
+            nc.gpsimd.dma_start(
+                out=tab_sc[32 * q : 32 * q + 8, :].bitcast(I32), in_=tab_scales[:, 4 * q : 4 * q + 4, :].bitcast(I32)
+            )
+        nc.sync.dma_start(list1[:], offs)
+        nc.sync.dma_start(out=tab[0][:], in_=tab_words[0].rearrange("p t i -> p (t i)").bitcast(I32))
+        w1_first = [load(f"w1_first{a}", pass_rows(w1, a)[:, :, 0:P], W1_FIRST + 2 * a) for a in range(2)]
+        nc.sync.dma_start(out=tab[1][:], in_=tab_words[1].rearrange("p t i -> p (t i)").bitcast(I32))
+        nc.sync.dma_start(list2[:], offs2)
+        nc.sync.dma_start(out=wgs_rows[:, 0:BANK], in_=wgs[:, 0:BANK])
+        load_page(0)
+        nc.sync.dma_start(out=wgs_rows[:, BANK:], in_=wgs[:, BANK:])
+        nc.sync.dma_start(list3[:], offs3)
+        w1_rest = [load(f"w1_rest{a}", pass_rows(w1, a)[:, :, P:K_PASS], W1_REST + 6 * a) for a in range(2)]
+        load_page(1)
+        w1_upper = [load(f"w1_upper{a}", pass_rows(w1, a)[:, :, K_PASS:], W1_UPPER + 8 * a) for a in range(2)]
+        load_page(2)
+
+        v_codes = [own("v_codes0", [P, S], U32)]
+        nc.vector.tensor_copy(v_codes[0][:], tab[0][:].bitcast(U32).indirect(list1[:]))
+        nc.vector.tensor_copy(v_sc[:], tab_sc[:].indirect(list1[:]))
+
+        wp_raw = [load(f"wp_raw{a}", pass_rows(wp, a), TAB + 8 * a) for a in range(2)]
+        load_page(3)
+        wgs_planes = placed("wgs_planes", [P, PACK, S], F32, WGS_PLANES)
+        for q in (0, 2, 1, 3):
+            nc.sync.dma_start(
+                out=wgs_planes[32 * q : 32 * q + 32, :, :], in_=wgs.rearrange("(q i) j -> q i j", i=PACK)
+            )
+        nc.sync.dma_start(out=wb_codes[:].bitcast(I32), in_=wb_words.rearrange("a p c -> p a c").bitcast(I32))
+        for q in range(QUADS):
+            nc.sync.dma_start(
+                out=wb_sc[32 * q : 32 * q + 4, :, :].bitcast(I32),
+                in_=wb_scales[:, 4 * q : 4 * q + 4, :].rearrange("a r c -> r a c").bitcast(I32),
+            )
+        load_page(4)
+
+        grouped = placed("g_first", [P, 2 * K_PASS], BF16, G_FIRST)
+        for a in range(2):
+            nc.scalar.copy(out=woven(grouped[:, a * K_PASS : (a + 1) * K_PASS]), in_=planar(w1_first[a][:]))
+        w1_q = {}
+        codes, scales = quantize("w1_first", grouped[:], 2 * K_PASS)
+        for a in range(2):
+            w1_q[0, a] = (codes[:, a * P : (a + 1) * P], scales[:, a * P : (a + 1) * P])
+
+        v_codes.append(placed("v_codes1", [P, S], U32, TAB_SC))
+        for u in range(2):
+            nc.vector.tensor_copy(
+                v_codes[1][:, u * BANK : (u + 1) * BANK],
+                tab[1][:].bitcast(U32).indirect(list1[:, u * 32 : (u + 1) * 32]),
+            )
+
+        def h_half(index, u, dest):
+            cols = slice(u * BANK, (u + 1) * BANK)
+            bank = banks[(2 * index + u) % 8]
+            for a in range(2):
+                nc.tensor.matmul_mx(
+                    out=bank[:],
+                    lhsT=w1_q[index, a][0].bitcast(FP8X4),
+                    lhsT_scale=w1_q[index, a][1],
+                    rhs=v_codes[a][:, cols].bitcast(FP8X4),
+                    rhs_scale=v_sc[4 * a :, cols],
+                    start=(a == 0),
+                    stop=(a == 1),
+                )
+            nc.scalar.copy(out=dest, in_=bank[:])
+
+        hs = {}
+
+        def make_h(index):
+            kb = H1 + 4 * (index - 1) if index < 6 else W1_REST + 4 * (index - 6)
+            hs[index] = placed(f"h{index}", [P, S], F32, kb)
+            for u in range(2):
+                h_half(index, u, hs[index][:, u * BANK : (u + 1) * BANK])
+
+        for u in range(2):
+            half = placed(f"h0_{u}", [P, BANK], F32, (G_REST1 + 1, H0B)[u])
+            h_half(0, u, half[:])
+            nc.vector.tensor_tensor(
+                pages[0][:].indirect(list2[:, u * 32 : (u + 1) * 32]),
+                half[:],
+                wgs_rows[:, u * BANK : (u + 1) * BANK],
+                MULT,
+            )
+
+        for first, count, kb in ((1, 1, G_REST1), (2, 2, G_REST2)):
+            width = count * P
+            grouped = placed(f"g_rest{first}", [P, 2 * PACK * width], BF16, kb)
+            for a in range(2):
+                nc.scalar.copy(
+                    out=woven(grouped[:, a * PACK * width : (a + 1) * PACK * width]),
+                    in_=planar(w1_rest[a][:, :, (first - 1) * P : (first - 1) * P + width]),
+                )
+            codes, scales = quantize(f"w1_rest{first}", grouped[:], 2 * PACK * width)
+            for b in range(count):
+                for a in range(2):
+                    cols = slice(a * width + b * P, a * width + (b + 1) * P)
+                    w1_q[first + b, a] = (codes[:, cols], scales[:, cols])
+        for index in range(1, 4):
+            make_h(index)
+
+        for a in range(2):
+            grouped = placed(f"g_upper{a}", [P, PACK * K_PASS], BF16, G_UPPER + 4 * a)
+            nc.scalar.copy(
+                out=grouped[:].rearrange("p (t m j) -> p m j t", t=PACK, j=PACK),
+                in_=w1_upper[a][:].rearrange("p j (m t) -> p m j t", t=PACK),
+            )
+            codes, scales = quantize(f"w1_upper{a}", grouped[:], PACK * K_PASS)
+            for t in range(PACK):
+                w1_q[4 + t, a] = (codes[:, t * P : (t + 1) * P], scales[:, t * P : (t + 1) * P])
+        for index in range(4, 8):
+            make_h(index)
+
+        wp_grouped = []
+        for a in range(2):
+            wp_grouped.append(placed(f"g_wp{a}", [P, PACK * N], BF16, G_WP + 4 * a))
+            nc.scalar.copy(out=woven(wp_grouped[a][:]), in_=planar(wp_raw[a][:]))
+
+        x_planes = placed("x_planes", [P, PACK, SLOTS], BF16, TAB + 16)
+        for index in range(4):
+            if index > 0:
+                nc.vector.tensor_tensor(pages[index][:].indirect(list2[:]), hs[index][:], wgs_rows[:], MULT)
+            kb = (G_REST1, G_REST2 + 2, X_ROWS2, X_ROWS2 + 2)[index]
+            x_rows = placed(f"x_rows{index}", [P, SLOTS], BF16, kb)
+            nc.vector.tensor_copy(x_rows[:], pages[index][:].indirect(list3[:]))
+            nc.sync.dma_start(out=x_planes[32 * index : 32 * index + 32, :, :], in_=x_rows[:])
+        for index in range(5, 8):
+            load_page(index)
+        zg_low = []
+        for u in range(2):
+            zg_low.append(placed(f"zg_low{u}", [P, PACK * BANK], BF16, TAB + 24 + 4 * u))
+            nc.scalar.activation(woven(zg_low[u][:]), planar(x_planes[:, :, u * BANK : (u + 1) * BANK]), RELU)
+
+        nc.vector.tensor_tensor(pages[4][:].indirect(list2[:]), hs[4][:], wgs_planes[:, 0, :], MULT)
+        wp_q = [quantize(f"wp{a}", wp_grouped[a][:], PACK * N, H1 + 12 + 2 * a) for a in range(2)]
+        for t in range(1, PACK):
+            nc.vector.tensor_tensor(pages[4 + t][:].indirect(list2[:]), hs[4 + t][:], wgs_planes[:, t, :], MULT)
+
+        out_view = out.rearrange("(b p) m -> p b m", p=P)
+        chunks = SLOTS // CHUNK
+        x_late, z_low, z_high, brands = {}, {}, {}, {}
+
+        def multiply(c, a):
+            if a == 0:
+                codes, scales = z_low[c * CHUNK // BANK]
+                base = c * CHUNK % BANK
+            else:
+                codes, scales = z_high[c]
+                base = 0
+            for b in range(4):
+                u, e = divmod(b, 2)
+                for part in range(CHUNK // P):
+                    cols = slice(base + part * P, base + (part + 1) * P)
+                    nc.tensor.matmul_mx(
+                        out=banks[4 * (c % 2) + u][:, e * CHUNK + part * P : e * CHUNK + (part + 1) * P],
+                        lhsT=wb_codes[:, a, 2 * b * P : 2 * (b + 1) * P].bitcast(FP4X4),
+                        lhsT_scale=wb_sc[:, a, b * P : (b + 1) * P],
+                        rhs=codes[:, cols].bitcast(FP8X4),
+                        rhs_scale=scales[:, cols],
+                        start=(a == 0 and e == 0 and part == 0),
+                        stop=(a == 1 and e == 1 and part == CHUNK // P - 1),
+                    )
+            for b in range(4):
+                u, e = divmod(b, 2)
+                cols = slice(base, base + CHUNK)
+                nc.tensor.matmul_mx(
+                    out=banks[4 * (c % 2) + 2 + u][:, e * CHUNK : (e + 1) * CHUNK],
+                    lhsT=wp_q[a][0][:, b * P : (b + 1) * P].bitcast(FP8X4),
+                    lhsT_scale=wp_q[a][1][:, b * P : (b + 1) * P],
+                    rhs=codes[:, cols].bitcast(FP8X4),
+                    rhs_scale=scales[:, cols],
+                    start=(a == 0 and e == 0),
+                    stop=(a == 1 and e == 1),
+                )
+
+        def gather(c):
+            kb = (H7 + 2, WGS_PLANES, H7 + 2, W1_UPPER + 2)[c]
+            x_late[c] = placed(f"x_late{c}", [P, PACK, CHUNK], BF16, kb)
+            for t in range(PACK):
+                nc.vector.tensor_copy(
+                    x_late[c][:, t, :],
+                    pages[4 + t][:].indirect(list3[:, c * CHUNK // 16 : (c + 1) * CHUNK // 16]),
+                )
+
+        def quantize_chunk(c):
+            grouped = placed(f"zg_high{c}", [P, PACK * CHUNK], BF16, ZG_HIGH + 2 * c)
+            nc.scalar.activation(woven(grouped[:]), planar(x_late[c][:]), RELU)
+            z_high[c] = quantize(f"z_high{c}", grouped[:], PACK * CHUNK, W1_UPPER if c == 2 else None)
+
+        def copy_brand(c):
+            brands[c] = [placed(f"brand{c}_{u}", [P, BANK], F32, W1_UPPER + 4 * c + 2 * u) for u in range(2)]
+            for u in range(2):
+                nc.scalar.copy(out=brands[c][u][:], in_=banks[4 * (c % 2) + u][:])
+
+        def finish(c):
+            kb = (PAGES + 16, PAGES + 8, PAGES + 20, PAGES + 24)[c]
+            for u in range(2):
+                result = placed(f"result{c}_{u}", [P, BANK], F32, kb + 2 * u)
+                nc.vector.tensor_tensor(result[:], banks[4 * (c % 2) + 2 + u][:], brands[c][u][:], MAX)
+                nc.sync.dma_start(
+                    out=out_view[:, 2 * u : 2 * u + 2, c * CHUNK : (c + 1) * CHUNK],
+                    in_=result[:].rearrange("p (e m) -> p e m", e=2),
+                )
+
+        z_low[0] = quantize("z_low0", zg_low[0][:], PACK * BANK, H7)
+        multiply(0, 0)
+        multiply(1, 0)
+        gather(0)
+        gather(1)
+        quantize_chunk(0)
+        multiply(0, 1)
+        copy_brand(0)
+        gather(2)
+        quantize_chunk(1)
+        multiply(1, 1)
+        copy_brand(1)
+        z_low[1] = quantize("z_low1", zg_low[1][:], PACK * BANK, ZG_HIGH)
+        finish(0)
+        multiply(2, 0)
+        quantize_chunk(2)
+        multiply(2, 1)
+        gather(3)
+        quantize_chunk(3)
+        finish(1)
+        copy_brand(2)
+        multiply(3, 0)
+        multiply(3, 1)
+        copy_brand(3)
+        finish(2)
+        finish(3)

@@ -23,9 +23,9 @@ K_PASS = P * PACK
 BANK = 512
 CHUNK = 256
 QUADS = 4
-
-
 KB = 1024
+
+TAB, TAB_SC, PAGES, W1_RAW, PLANES, H_TILES, GROUPED, X_PLANES = 0, 32, 36, 84, 116, 132, 164, 180
 
 
 def tile_list_slot_bidding_kernel(
@@ -45,10 +45,6 @@ def tile_list_slot_bidding_kernel(
         def placed(name, shape, dtype, kb):
             return shared.tile(shape, dtype, name=name, align_bytes=64, offset=kb * KB)
 
-        TAB, TAB_SC, PAGES, W1_FIRST, W1_REST, W1_UPPER, WGS_PLANES = 0, 32, 36, 84, 88, 100, 116
-        G_FIRST, G_REST1, G_REST2, G_UPPER, H0B, H1, X_ROWS2, ZG_HIGH, G_WP = 132, 134, 136, 140, 148, 150, 170, 174, 182
-        H7 = W1_REST + 4
-
         list1 = lists.tile([P, S // 16], U16, name="list1")
         list2 = lists.tile([P, S // 16], U16, name="list2")
         list3 = lists.tile([P, SLOTS // 16], U16, name="list3")
@@ -65,7 +61,8 @@ def tile_list_slot_bidding_kernel(
         pages = {}
 
         def load_page(index):
-            pages[index] = placed(f"page{index}", [P, T2], F32, PAGES + 8 * (index % 6))
+            kb = PAGES + 8 * index if index < 6 else TAB + 16 + 8 * (index - 6)
+            pages[index] = placed(f"page{index}", [P, T2], F32, kb)
             if index < 4:
                 rows = page0[index * P : (index + 1) * P, :]
             else:
@@ -76,6 +73,11 @@ def tile_list_slot_bidding_kernel(
             raw = placed(name, list(rows.shape), F32, kb)
             nc.sync.dma_start(out=raw[:], in_=rows)
             return raw
+
+        def load_w1(name, first, last):
+            kb = W1_RAW + first // 32
+            width_kb = (last - first) // 64
+            return [load(f"{name}{a}", pass_rows(w1, a)[:, :, first:last], kb + width_kb * a) for a in range(2)]
 
         def quantize(name, grouped, width, kb=None):
             shape = [P, width // PACK]
@@ -98,50 +100,62 @@ def tile_list_slot_bidding_kernel(
             )
         nc.sync.dma_start(list1[:], offs)
         nc.sync.dma_start(out=tab[0][:], in_=tab_words[0].rearrange("p t i -> p (t i)").bitcast(I32))
-        w1_first = [load(f"w1_first{a}", pass_rows(w1, a)[:, :, 0:P], W1_FIRST + 2 * a) for a in range(2)]
+        w1_a = load_w1("w1_a", 0, P)
         nc.sync.dma_start(out=tab[1][:], in_=tab_words[1].rearrange("p t i -> p (t i)").bitcast(I32))
         nc.sync.dma_start(list2[:], offs2)
         nc.sync.dma_start(out=wgs_rows[:, 0:BANK], in_=wgs[:, 0:BANK])
         load_page(0)
+        w1_b = load_w1("w1_b", P, 2 * P)
         nc.sync.dma_start(out=wgs_rows[:, BANK:], in_=wgs[:, BANK:])
         nc.sync.dma_start(list3[:], offs3)
-        w1_rest = [load(f"w1_rest{a}", pass_rows(w1, a)[:, :, P:K_PASS], W1_REST + 6 * a) for a in range(2)]
         load_page(1)
-        w1_upper = [load(f"w1_upper{a}", pass_rows(w1, a)[:, :, K_PASS:], W1_UPPER + 8 * a) for a in range(2)]
+        w1_c = load_w1("w1_c", 2 * P, K_PASS)
         load_page(2)
+        load_page(3)
+        w1_d = load_w1("w1_d", K_PASS, H)
+        wgs_planes = placed("wgs_planes", [P, PACK, S], F32, PLANES)
+        for q in (0, 2, 1, 3):
+            nc.sync.dma_start(
+                out=wgs_planes[32 * q : 32 * q + 32, :, :], in_=wgs.rearrange("(q i) j -> q i j", i=PACK)
+            )
+        load_page(4)
+        load_page(5)
 
         v_codes = [own("v_codes0", [P, S], U32)]
         nc.vector.tensor_copy(v_codes[0][:], tab[0][:].bitcast(U32).indirect(list1[:]))
         nc.vector.tensor_copy(v_sc[:], tab_sc[:].indirect(list1[:]))
 
-        wp_raw = [load(f"wp_raw{a}", pass_rows(wp, a), TAB + 8 * a) for a in range(2)]
-        load_page(3)
-        wgs_planes = placed("wgs_planes", [P, PACK, S], F32, WGS_PLANES)
-        for q in (0, 2, 1, 3):
-            nc.sync.dma_start(
-                out=wgs_planes[32 * q : 32 * q + 32, :, :], in_=wgs.rearrange("(q i) j -> q i j", i=PACK)
-            )
-        nc.sync.dma_start(out=wb_codes[:].bitcast(I32), in_=wb_words.rearrange("a p c -> p a c").bitcast(I32))
-        for q in range(QUADS):
-            nc.sync.dma_start(
-                out=wb_sc[32 * q : 32 * q + 4, :, :].bitcast(I32),
-                in_=wb_scales[:, 4 * q : 4 * q + 4, :].rearrange("a r c -> r a c").bitcast(I32),
-            )
-        load_page(4)
-
-        grouped = placed("g_first", [P, 2 * K_PASS], BF16, G_FIRST)
-        for a in range(2):
-            nc.scalar.copy(out=woven(grouped[:, a * K_PASS : (a + 1) * K_PASS]), in_=planar(w1_first[a][:]))
         w1_q = {}
-        codes, scales = quantize("w1_first", grouped[:], 2 * K_PASS)
-        for a in range(2):
-            w1_q[0, a] = (codes[:, a * P : (a + 1) * P], scales[:, a * P : (a + 1) * P])
+
+        def quantize_w1(name, raw, first_tile, count):
+            width = count * P
+            grouped = placed("g_" + name, [P, 2 * PACK * width], BF16, GROUPED + 2 * first_tile)
+            for a in range(2):
+                nc.scalar.copy(out=woven(grouped[:, a * PACK * width : (a + 1) * PACK * width]), in_=planar(raw[a][:]))
+            codes, scales = quantize(name, grouped[:], 2 * PACK * width)
+            for b in range(count):
+                for a in range(2):
+                    cols = slice(a * width + b * P, a * width + (b + 1) * P)
+                    w1_q[first_tile + b, a] = (codes[:, cols], scales[:, cols])
+
+        quantize_w1("w1_a", w1_a, 0, 1)
 
         v_codes.append(placed("v_codes1", [P, S], U32, TAB_SC))
         for u in range(2):
             nc.vector.tensor_copy(
                 v_codes[1][:, u * BANK : (u + 1) * BANK],
                 tab[1][:].bitcast(U32).indirect(list1[:, u * 32 : (u + 1) * 32]),
+            )
+
+        wp_raw = [load("wp_raw0", pass_rows(wp, 0), TAB)]
+        load_page(6)
+        load_page(7)
+        wp_raw.append(load("wp_raw1", pass_rows(wp, 1), TAB + 8))
+        nc.sync.dma_start(out=wb_codes[:].bitcast(I32), in_=wb_words.rearrange("a p c -> p a c").bitcast(I32))
+        for q in range(QUADS):
+            nc.sync.dma_start(
+                out=wb_sc[32 * q : 32 * q + 4, :, :].bitcast(I32),
+                in_=wb_scales[:, 4 * q : 4 * q + 4, :].rearrange("a r c -> r a c").bitcast(I32),
             )
 
         def h_half(index, u, dest):
@@ -162,13 +176,14 @@ def tile_list_slot_bidding_kernel(
         hs = {}
 
         def make_h(index):
-            kb = H1 + 4 * (index - 1) if index < 6 else W1_REST + 4 * (index - 6)
-            hs[index] = placed(f"h{index}", [P, S], F32, kb)
+            hs[index] = placed(f"h{index}", [P, S], F32, H_TILES + 4 * index)
             for u in range(2):
                 h_half(index, u, hs[index][:, u * BANK : (u + 1) * BANK])
 
         for u in range(2):
-            half = placed(f"h0_{u}", [P, BANK], F32, (G_REST1 + 1, H0B)[u])
+            if u == 1:
+                quantize_w1("w1_b", w1_b, 1, 1)
+            half = placed(f"h0_{u}", [P, BANK], F32, (H_TILES, W1_RAW + 6)[u])
             h_half(0, u, half[:])
             nc.vector.tensor_tensor(
                 pages[0][:].indirect(list2[:, u * 32 : (u + 1) * 32]),
@@ -177,62 +192,56 @@ def tile_list_slot_bidding_kernel(
                 MULT,
             )
 
-        for first, count, kb in ((1, 1, G_REST1), (2, 2, G_REST2)):
-            width = count * P
-            grouped = placed(f"g_rest{first}", [P, 2 * PACK * width], BF16, kb)
-            for a in range(2):
-                nc.scalar.copy(
-                    out=woven(grouped[:, a * PACK * width : (a + 1) * PACK * width]),
-                    in_=planar(w1_rest[a][:, :, (first - 1) * P : (first - 1) * P + width]),
-                )
-            codes, scales = quantize(f"w1_rest{first}", grouped[:], 2 * PACK * width)
-            for b in range(count):
-                for a in range(2):
-                    cols = slice(a * width + b * P, a * width + (b + 1) * P)
-                    w1_q[first + b, a] = (codes[:, cols], scales[:, cols])
-        for index in range(1, 4):
-            make_h(index)
+        make_h(1)
+        quantize_w1("w1_c", w1_c, 2, 2)
+        make_h(2)
+        make_h(3)
 
         for a in range(2):
-            grouped = placed(f"g_upper{a}", [P, PACK * K_PASS], BF16, G_UPPER + 4 * a)
+            grouped = placed(f"g_w1_d{a}", [P, PACK * K_PASS], BF16, GROUPED + 8 + 4 * a)
             nc.scalar.copy(
                 out=grouped[:].rearrange("p (t m j) -> p m j t", t=PACK, j=PACK),
-                in_=w1_upper[a][:].rearrange("p j (m t) -> p m j t", t=PACK),
+                in_=w1_d[a][:].rearrange("p j (m t) -> p m j t", t=PACK),
             )
-            codes, scales = quantize(f"w1_upper{a}", grouped[:], PACK * K_PASS)
+            codes, scales = quantize(f"w1_d{a}", grouped[:], PACK * K_PASS)
             for t in range(PACK):
                 w1_q[4 + t, a] = (codes[:, t * P : (t + 1) * P], scales[:, t * P : (t + 1) * P])
         for index in range(4, 8):
             make_h(index)
 
-        wp_grouped = []
-        for a in range(2):
-            wp_grouped.append(placed(f"g_wp{a}", [P, PACK * N], BF16, G_WP + 4 * a))
-            nc.scalar.copy(out=woven(wp_grouped[a][:]), in_=planar(wp_raw[a][:]))
-
-        x_planes = placed("x_planes", [P, PACK, SLOTS], BF16, TAB + 16)
+        x_planes = placed("x_planes", [P, PACK, SLOTS], BF16, X_PLANES)
         for index in range(4):
             if index > 0:
                 nc.vector.tensor_tensor(pages[index][:].indirect(list2[:]), hs[index][:], wgs_rows[:], MULT)
-            kb = (G_REST1, G_REST2 + 2, X_ROWS2, X_ROWS2 + 2)[index]
-            x_rows = placed(f"x_rows{index}", [P, SLOTS], BF16, kb)
+            x_rows = placed(f"x_rows{index}", [P, SLOTS], BF16, W1_RAW + (12, 14, 24, 26)[index])
             nc.vector.tensor_copy(x_rows[:], pages[index][:].indirect(list3[:]))
             nc.sync.dma_start(out=x_planes[32 * index : 32 * index + 32, :, :], in_=x_rows[:])
-        for index in range(5, 8):
-            load_page(index)
+        wp_grouped = []
+
+        def cast_wp(a):
+            wp_grouped.append(placed(f"g_wp{a}", [P, PACK * N], BF16, GROUPED + 4 * a))
+            nc.scalar.copy(out=woven(wp_grouped[a][:]), in_=planar(wp_raw[a][:]))
+
+        cast_wp(0)
         zg_low = []
         for u in range(2):
-            zg_low.append(placed(f"zg_low{u}", [P, PACK * BANK], BF16, TAB + 24 + 4 * u))
+            zg_low.append(placed(f"zg_low{u}", [P, PACK * BANK], BF16, TAB + 4 * u))
             nc.scalar.activation(woven(zg_low[u][:]), planar(x_planes[:, :, u * BANK : (u + 1) * BANK]), RELU)
+        cast_wp(1)
 
-        nc.vector.tensor_tensor(pages[4][:].indirect(list2[:]), hs[4][:], wgs_planes[:, 0, :], MULT)
-        wp_q = [quantize(f"wp{a}", wp_grouped[a][:], PACK * N, H1 + 12 + 2 * a) for a in range(2)]
-        for t in range(1, PACK):
+        def scatter(t):
             nc.vector.tensor_tensor(pages[4 + t][:].indirect(list2[:]), hs[4 + t][:], wgs_planes[:, t, :], MULT)
 
+        scatter(0)
+        scatter(1)
+        wp_q = [quantize("wp0", wp_grouped[0][:], PACK * N)]
+        scatter(2)
+        z_low = [quantize("z_low0", zg_low[0][:], PACK * BANK)]
+        scatter(3)
+        z_low.append(quantize("z_low1", zg_low[1][:], PACK * BANK))
+
         out_view = out.rearrange("(b p) m -> p b m", p=P)
-        chunks = SLOTS // CHUNK
-        x_late, z_low, z_high, brands = {}, {}, {}, {}
+        x_late, zg_high, z_high, brands = {}, {}, {}, {}
 
         def multiply(c, a):
             if a == 0:
@@ -241,34 +250,48 @@ def tile_list_slot_bidding_kernel(
             else:
                 codes, scales = z_high[c]
                 base = 0
-            for b in range(4):
-                u, e = divmod(b, 2)
-                for part in range(CHUNK // P):
-                    cols = slice(base + part * P, base + (part + 1) * P)
+
+            def brand(u):
+                for e in range(2):
+                    b = 2 * u + e
+                    for part in range(CHUNK // P):
+                        cols = slice(base + part * P, base + (part + 1) * P)
+                        nc.tensor.matmul_mx(
+                            out=banks[4 * (c % 2) + u][:, e * CHUNK + part * P : e * CHUNK + (part + 1) * P],
+                            lhsT=wb_codes[:, a, 2 * b * P : 2 * (b + 1) * P].bitcast(FP4X4),
+                            lhsT_scale=wb_sc[:, a, b * P : (b + 1) * P],
+                            rhs=codes[:, cols].bitcast(FP8X4),
+                            rhs_scale=scales[:, cols],
+                            start=(a == 0 and e == 0 and part == 0),
+                            stop=(a == 1 and e == 1 and part == CHUNK // P - 1),
+                        )
+
+            def perf(u):
+                for e in range(2):
+                    b = 2 * u + e
+                    cols = slice(base, base + CHUNK)
                     nc.tensor.matmul_mx(
-                        out=banks[4 * (c % 2) + u][:, e * CHUNK + part * P : e * CHUNK + (part + 1) * P],
-                        lhsT=wb_codes[:, a, 2 * b * P : 2 * (b + 1) * P].bitcast(FP4X4),
-                        lhsT_scale=wb_sc[:, a, b * P : (b + 1) * P],
+                        out=banks[4 * (c % 2) + 2 + u][:, e * CHUNK : (e + 1) * CHUNK],
+                        lhsT=wp_q[a][0][:, b * P : (b + 1) * P].bitcast(FP8X4),
+                        lhsT_scale=wp_q[a][1][:, b * P : (b + 1) * P],
                         rhs=codes[:, cols].bitcast(FP8X4),
                         rhs_scale=scales[:, cols],
-                        start=(a == 0 and e == 0 and part == 0),
-                        stop=(a == 1 and e == 1 and part == CHUNK // P - 1),
+                        start=(a == 0 and e == 0),
+                        stop=(a == 1 and e == 1),
                     )
-            for b in range(4):
-                u, e = divmod(b, 2)
-                cols = slice(base, base + CHUNK)
-                nc.tensor.matmul_mx(
-                    out=banks[4 * (c % 2) + 2 + u][:, e * CHUNK : (e + 1) * CHUNK],
-                    lhsT=wp_q[a][0][:, b * P : (b + 1) * P].bitcast(FP8X4),
-                    lhsT_scale=wp_q[a][1][:, b * P : (b + 1) * P],
-                    rhs=codes[:, cols].bitcast(FP8X4),
-                    rhs_scale=scales[:, cols],
-                    start=(a == 0 and e == 0),
-                    stop=(a == 1 and e == 1),
-                )
+
+            if a == 0:
+                brand(0)
+                brand(1)
+                perf(0)
+                perf(1)
+            else:
+                for u in range(2):
+                    brand(u)
+                    perf(u)
 
         def gather(c):
-            kb = (H7 + 2, WGS_PLANES, H7 + 2, W1_UPPER + 2)[c]
+            kb = X_PLANES + (0, 2, 0, 0)[c]
             x_late[c] = placed(f"x_late{c}", [P, PACK, CHUNK], BF16, kb)
             for t in range(PACK):
                 nc.vector.tensor_copy(
@@ -276,48 +299,52 @@ def tile_list_slot_bidding_kernel(
                     pages[4 + t][:].indirect(list3[:, c * CHUNK // 16 : (c + 1) * CHUNK // 16]),
                 )
 
+        def rectify(c):
+            zg_high[c] = placed(f"zg_high{c}", [P, PACK * CHUNK], BF16, GROUPED + 8 + 2 * c)
+            nc.scalar.activation(woven(zg_high[c][:]), planar(x_late[c][:]), RELU)
+
         def quantize_chunk(c):
-            grouped = placed(f"zg_high{c}", [P, PACK * CHUNK], BF16, ZG_HIGH + 2 * c)
-            nc.scalar.activation(woven(grouped[:]), planar(x_late[c][:]), RELU)
-            z_high[c] = quantize(f"z_high{c}", grouped[:], PACK * CHUNK, W1_UPPER if c == 2 else None)
+            z_high[c] = quantize(f"z_high{c}", zg_high[c][:], PACK * CHUNK)
 
         def copy_brand(c):
-            brands[c] = [placed(f"brand{c}_{u}", [P, BANK], F32, W1_UPPER + 4 * c + 2 * u) for u in range(2)]
+            brands[c] = [placed(f"brand{c}_{u}", [P, BANK], F32, W1_RAW + 4 * c + 2 * u) for u in range(2)]
             for u in range(2):
                 nc.scalar.copy(out=brands[c][u][:], in_=banks[4 * (c % 2) + u][:])
 
         def finish(c):
-            kb = (PAGES + 16, PAGES + 8, PAGES + 20, PAGES + 24)[c]
             for u in range(2):
-                result = placed(f"result{c}_{u}", [P, BANK], F32, kb + 2 * u)
+                result = placed(f"result{c}_{u}", [P, BANK], F32, W1_RAW + 16 + 4 * c + 2 * u)
                 nc.vector.tensor_tensor(result[:], banks[4 * (c % 2) + 2 + u][:], brands[c][u][:], MAX)
                 nc.sync.dma_start(
                     out=out_view[:, 2 * u : 2 * u + 2, c * CHUNK : (c + 1) * CHUNK],
                     in_=result[:].rearrange("p (e m) -> p e m", e=2),
                 )
 
-        z_low[0] = quantize("z_low0", zg_low[0][:], PACK * BANK, H7)
         multiply(0, 0)
         multiply(1, 0)
         gather(0)
+        wp_q.append(quantize("wp1", wp_grouped[1][:], PACK * N))
         gather(1)
+        rectify(0)
         quantize_chunk(0)
+        rectify(1)
         multiply(0, 1)
         copy_brand(0)
         gather(2)
         quantize_chunk(1)
         multiply(1, 1)
-        copy_brand(1)
-        z_low[1] = quantize("z_low1", zg_low[1][:], PACK * BANK, ZG_HIGH)
         finish(0)
         multiply(2, 0)
+        rectify(2)
         quantize_chunk(2)
+        copy_brand(1)
         multiply(2, 1)
         gather(3)
-        quantize_chunk(3)
         finish(1)
-        copy_brand(2)
         multiply(3, 0)
+        rectify(3)
+        quantize_chunk(3)
+        copy_brand(2)
         multiply(3, 1)
         copy_brand(3)
         finish(2)

@@ -147,10 +147,8 @@ def tile_list_slot_bidding_kernel(
                 tab[1][:].bitcast(U32).indirect(list1[:, u * 32 : (u + 1) * 32]),
             )
 
-        wp_raw = [load("wp_raw0", pass_rows(wp, 0), TAB)]
         load_page(6)
-        load_page(7)
-        wp_raw.append(load("wp_raw1", pass_rows(wp, 1), TAB + 8))
+        wp_raw = [load(f"wp_raw{a}", pass_rows(wp, a), TAB + 8 * a) for a in range(2)]
         nc.sync.dma_start(out=wb_codes[:].bitcast(I32), in_=wb_words.rearrange("a p c -> p a c").bitcast(I32))
         for q in range(QUADS):
             nc.sync.dma_start(
@@ -175,8 +173,8 @@ def tile_list_slot_bidding_kernel(
 
         hs = {}
 
-        def make_h(index):
-            hs[index] = placed(f"h{index}", [P, S], F32, H_TILES + 4 * index)
+        def make_h(index, kb=None):
+            hs[index] = placed(f"h{index}", [P, S], F32, H_TILES + 4 * index if kb is None else kb)
             for u in range(2):
                 h_half(index, u, hs[index][:, u * BANK : (u + 1) * BANK])
 
@@ -197,16 +195,20 @@ def tile_list_slot_bidding_kernel(
         make_h(2)
         make_h(3)
 
+        grouped = placed("g_w1_d", [P, 2 * PACK * K_PASS], BF16, GROUPED + 8)
         for a in range(2):
-            grouped = placed(f"g_w1_d{a}", [P, PACK * K_PASS], BF16, GROUPED + 8 + 4 * a)
             nc.scalar.copy(
-                out=grouped[:].rearrange("p (t m j) -> p m j t", t=PACK, j=PACK),
+                out=grouped[:, a * PACK * K_PASS : (a + 1) * PACK * K_PASS].rearrange(
+                    "p (t m j) -> p m j t", t=PACK, j=PACK
+                ),
                 in_=w1_d[a][:].rearrange("p j (m t) -> p m j t", t=PACK),
             )
-            codes, scales = quantize(f"w1_d{a}", grouped[:], PACK * K_PASS)
+        codes, scales = quantize("w1_d", grouped[:], 2 * PACK * K_PASS)
+        for a in range(2):
             for t in range(PACK):
-                w1_q[4 + t, a] = (codes[:, t * P : (t + 1) * P], scales[:, t * P : (t + 1) * P])
-        for index in range(4, 8):
+                cols = slice(a * K_PASS + t * P, a * K_PASS + (t + 1) * P)
+                w1_q[4 + t, a] = (codes[:, cols], scales[:, cols])
+        for index in range(4, 7):
             make_h(index)
 
         x_planes = placed("x_planes", [P, PACK, SLOTS], BF16, X_PLANES)
@@ -216,88 +218,83 @@ def tile_list_slot_bidding_kernel(
             x_rows = placed(f"x_rows{index}", [P, SLOTS], BF16, W1_RAW + (12, 14, 24, 26)[index])
             nc.vector.tensor_copy(x_rows[:], pages[index][:].indirect(list3[:]))
             nc.sync.dma_start(out=x_planes[32 * index : 32 * index + 32, :, :], in_=x_rows[:])
-        wp_grouped = []
-
-        def cast_wp(a):
-            wp_grouped.append(placed(f"g_wp{a}", [P, PACK * N], BF16, GROUPED + 4 * a))
-            nc.scalar.copy(out=woven(wp_grouped[a][:]), in_=planar(wp_raw[a][:]))
-
-        cast_wp(0)
-        zg_low = []
-        for u in range(2):
-            zg_low.append(placed(f"zg_low{u}", [P, PACK * BANK], BF16, TAB + 4 * u))
-            nc.scalar.activation(woven(zg_low[u][:]), planar(x_planes[:, :, u * BANK : (u + 1) * BANK]), RELU)
-        cast_wp(1)
+        load_page(7)
 
         def scatter(t):
             nc.vector.tensor_tensor(pages[4 + t][:].indirect(list2[:]), hs[4 + t][:], wgs_planes[:, t, :], MULT)
 
-        scatter(0)
-        scatter(1)
-        wp_q = [quantize("wp0", wp_grouped[0][:], PACK * N)]
-        scatter(2)
-        z_low = [quantize("z_low0", zg_low[0][:], PACK * BANK)]
-        scatter(3)
+        for t in range(3):
+            scatter(t)
+
+        wp_grouped = placed("g_wp", [P, 2 * PACK * N], BF16, GROUPED)
+        for a in range(2):
+            nc.scalar.copy(out=woven(wp_grouped[:, a * PACK * N : (a + 1) * PACK * N]), in_=planar(wp_raw[a][:]))
+        wp_codes, wp_sc = quantize("wp", wp_grouped[:], 2 * PACK * N)
+
+        zg_low, z_low = [], []
+        for u in range(2):
+            zg_low.append(placed(f"zg_low{u}", [P, PACK * BANK], BF16, TAB + 4 * u))
+            nc.scalar.activation(woven(zg_low[u][:]), planar(x_planes[:, :, u * BANK : (u + 1) * BANK]), RELU)
+        z_low.append(quantize("z_low0", zg_low[0][:], PACK * BANK, H_TILES + 28))
+        make_h(7, TAB)
         z_low.append(quantize("z_low1", zg_low[1][:], PACK * BANK))
 
         out_view = out.rearrange("(b p) m -> p b m", p=P)
         x_late, zg_high, z_high, brands = {}, {}, {}, {}
+        brand_bank = (0, 4, 0, 0)
+        perf_bank = (2, 6, 4, 2)
 
-        def multiply(c, a):
+        def z_operand(c, a):
             if a == 0:
                 codes, scales = z_low[c * CHUNK // BANK]
-                base = c * CHUNK % BANK
-            else:
-                codes, scales = z_high[c]
-                base = 0
+                return codes, scales, c * CHUNK % BANK
+            codes, scales = z_high[c]
+            return codes, scales, 0
 
-            def brand(u):
-                for e in range(2):
-                    b = 2 * u + e
-                    for part in range(CHUNK // P):
-                        cols = slice(base + part * P, base + (part + 1) * P)
-                        nc.tensor.matmul_mx(
-                            out=banks[4 * (c % 2) + u][:, e * CHUNK + part * P : e * CHUNK + (part + 1) * P],
-                            lhsT=wb_codes[:, a, 2 * b * P : 2 * (b + 1) * P].bitcast(FP4X4),
-                            lhsT_scale=wb_sc[:, a, b * P : (b + 1) * P],
-                            rhs=codes[:, cols].bitcast(FP8X4),
-                            rhs_scale=scales[:, cols],
-                            start=(a == 0 and e == 0 and part == 0),
-                            stop=(a == 1 and e == 1 and part == CHUNK // P - 1),
-                        )
-
-            def perf(u):
-                for e in range(2):
-                    b = 2 * u + e
-                    cols = slice(base, base + CHUNK)
+        def brand(c, a, u):
+            codes, scales, base = z_operand(c, a)
+            for e in range(2):
+                b = 2 * u + e
+                for part in range(CHUNK // P):
+                    cols = slice(base + part * P, base + (part + 1) * P)
                     nc.tensor.matmul_mx(
-                        out=banks[4 * (c % 2) + 2 + u][:, e * CHUNK : (e + 1) * CHUNK],
-                        lhsT=wp_q[a][0][:, b * P : (b + 1) * P].bitcast(FP8X4),
-                        lhsT_scale=wp_q[a][1][:, b * P : (b + 1) * P],
+                        out=banks[brand_bank[c] + u][:, e * CHUNK + part * P : e * CHUNK + (part + 1) * P],
+                        lhsT=wb_codes[:, a, 2 * b * P : 2 * (b + 1) * P].bitcast(FP4X4),
+                        lhsT_scale=wb_sc[:, a, b * P : (b + 1) * P],
                         rhs=codes[:, cols].bitcast(FP8X4),
                         rhs_scale=scales[:, cols],
-                        start=(a == 0 and e == 0),
-                        stop=(a == 1 and e == 1),
+                        start=(a == 0 and e == 0 and part == 0),
+                        stop=(a == 1 and e == 1 and part == CHUNK // P - 1),
                     )
 
-            if a == 0:
-                brand(0)
-                brand(1)
-                perf(0)
-                perf(1)
-            else:
-                for u in range(2):
-                    brand(u)
-                    perf(u)
-
-        def gather(c):
-            kb = X_PLANES + (0, 2, 0, 0)[c]
-            x_late[c] = placed(f"x_late{c}", [P, PACK, CHUNK], BF16, kb)
-            for t in range(PACK):
-                nc.vector.tensor_copy(
-                    x_late[c][:, t, :],
-                    pages[4 + t][:].indirect(list3[:, c * CHUNK // 16 : (c + 1) * CHUNK // 16]),
+        def perf(c, a, u):
+            codes, scales, base = z_operand(c, a)
+            for e in range(2):
+                b = 2 * u + e
+                cols = slice(base, base + CHUNK)
+                w_cols = slice(a * N + b * P, a * N + (b + 1) * P)
+                nc.tensor.matmul_mx(
+                    out=banks[perf_bank[c] + u][:, e * CHUNK : (e + 1) * CHUNK],
+                    lhsT=wp_codes[:, w_cols].bitcast(FP8X4),
+                    lhsT_scale=wp_sc[:, w_cols],
+                    rhs=codes[:, cols].bitcast(FP8X4),
+                    rhs_scale=scales[:, cols],
+                    start=(a == 0 and e == 0),
+                    stop=(a == 1 and e == 1),
                 )
+
+        def multiply(c, a):
+            for product in (brand, perf):
+                for u in range(2):
+                    product(c, a, u)
+
+        def gather(c, t):
+            if t == 0:
+                x_late[c] = placed(f"x_late{c}", [P, PACK, CHUNK], BF16, (X_PLANES, H_TILES + 28)[c % 2])
+            nc.vector.tensor_copy(
+                x_late[c][:, t, :],
+                pages[4 + t][:].indirect(list3[:, c * CHUNK // 16 : (c + 1) * CHUNK // 16]),
+            )
 
         def rectify(c):
             zg_high[c] = placed(f"zg_high{c}", [P, PACK * CHUNK], BF16, GROUPED + 8 + 2 * c)
@@ -306,46 +303,57 @@ def tile_list_slot_bidding_kernel(
         def quantize_chunk(c):
             z_high[c] = quantize(f"z_high{c}", zg_high[c][:], PACK * CHUNK)
 
-        def copy_brand(c):
-            brands[c] = [placed(f"brand{c}_{u}", [P, BANK], F32, W1_RAW + 4 * c + 2 * u) for u in range(2)]
+        def copy_first(c):
+            brands[c] = [placed(f"first{c}_{u}", [P, BANK], F32, W1_RAW + 4 * c + 2 * u) for u in range(2)]
             for u in range(2):
-                nc.scalar.copy(out=brands[c][u][:], in_=banks[4 * (c % 2) + u][:])
+                nc.scalar.copy(out=brands[c][u][:], in_=banks[(perf_bank if c == 3 else brand_bank)[c] + u][:])
 
         def finish(c):
+            result = placed(f"result{c}", [P, 2, BANK], F32, (X_PLANES, H_TILES + 28, W1_RAW + 24, W1_RAW + 28)[c])
             for u in range(2):
-                result = placed(f"result{c}_{u}", [P, BANK], F32, W1_RAW + 16 + 4 * c + 2 * u)
-                nc.vector.tensor_tensor(result[:], banks[4 * (c % 2) + 2 + u][:], brands[c][u][:], MAX)
+                second = banks[(brand_bank if c == 3 else perf_bank)[c] + u]
+                nc.vector.tensor_tensor(result[:, u, :], second[:], brands[c][u][:], MAX)
                 nc.sync.dma_start(
                     out=out_view[:, 2 * u : 2 * u + 2, c * CHUNK : (c + 1) * CHUNK],
-                    in_=result[:].rearrange("p (e m) -> p e m", e=2),
+                    in_=result[:, u, :].rearrange("p (e m) -> p e m", e=2),
                 )
 
         multiply(0, 0)
         multiply(1, 0)
-        gather(0)
-        wp_q.append(quantize("wp1", wp_grouped[1][:], PACK * N))
-        gather(1)
+        for t in range(3):
+            gather(0, t)
+        scatter(3)
+        gather(1, 0)
+        gather(0, 3)
+        for t in range(1, PACK):
+            gather(1, t)
         rectify(0)
         quantize_chunk(0)
-        rectify(1)
         multiply(0, 1)
-        copy_brand(0)
-        gather(2)
+        rectify(1)
+        gather(2, 0)
+        gather(2, 1)
         quantize_chunk(1)
         multiply(1, 1)
-        finish(0)
-        multiply(2, 0)
+        gather(2, 2)
+        gather(2, 3)
+        copy_first(0)
         rectify(2)
+        for t in range(PACK):
+            gather(3, t)
+        copy_first(1)
+        multiply(2, 0)
         quantize_chunk(2)
-        copy_brand(1)
         multiply(2, 1)
-        gather(3)
-        finish(1)
-        multiply(3, 0)
+        finish(0)
         rectify(3)
         quantize_chunk(3)
-        copy_brand(2)
-        multiply(3, 1)
-        copy_brand(3)
+        copy_first(2)
+        for product in (perf, brand):
+            for a in range(2):
+                for u in range(2):
+                    product(3, a, u)
+        finish(1)
         finish(2)
+        copy_first(3)
         finish(3)

@@ -50,7 +50,8 @@ def tile_list_slot_bidding_kernel(
         list3 = lists.tile([P, SLOTS // 16], U16, name="list3")
         tab = [placed(f"tab{a}", [P, T], I32, TAB + 16 * a) for a in range(2)]
         tab_sc = placed("tab_sc", [P, T], U8, TAB_SC)
-        v_sc = own("v_sc", [P, S], U8)
+        picked_sc = own("picked_sc", [P, S], U8)
+        v_sc = own("v_sc", [P, 2, S], U8)
         wb_codes = own("wb_codes", [P, 2, 2 * N], U8)
         wb_sc = own("wb_sc", [P, 2, N], U8)
         wgs_rows = own("wgs_rows", [P, S], F32)
@@ -92,12 +93,12 @@ def tile_list_slot_bidding_kernel(
         def planar(planes):
             return planes.rearrange("p j (c i) -> p c j i", i=4)
 
-        nc.vector.memset(tab_sc[:].bitcast(I32), 0)
+        for a in range(2):
+            nc.sync.dma_start(out=tab_sc[a:32:2, :].bitcast(I32), in_=tab_scales[a].bitcast(I32))
+        nc.vector.memset(tab_sc[32:64, :].bitcast(I32), 0)
+        nc.vector.memset(tab_sc[64:128, :].bitcast(I32), 0)
+        nc.vector.memset(v_sc[:].rearrange("p a c -> p (a c)").bitcast(I32), 0)
         nc.vector.memset(wb_sc[:].rearrange("p a c -> p (a c)").bitcast(I32), 0)
-        for q in range(QUADS):
-            nc.gpsimd.dma_start(
-                out=tab_sc[32 * q : 32 * q + 8, :].bitcast(I32), in_=tab_scales[:, 4 * q : 4 * q + 4, :].bitcast(I32)
-            )
         nc.sync.dma_start(list1[:], offs)
         nc.sync.dma_start(out=tab[0][:], in_=tab_words[0].rearrange("p t i -> p (t i)").bitcast(I32))
         w1_a = load_w1("w1_a", 0, P)
@@ -121,9 +122,13 @@ def tile_list_slot_bidding_kernel(
         load_page(4)
         load_page(5)
 
+        nc.vector.tensor_copy(picked_sc[:], tab_sc[:].indirect(list1[:]))
+        for q in range(QUADS):
+            nc.gpsimd.dma_start(
+                out=v_sc[32 * q : 32 * q + 4, :, :].bitcast(I32), in_=picked_sc[8 * q : 8 * q + 8, :].bitcast(I32)
+            )
         v_codes = [own("v_codes0", [P, S], U32)]
         nc.vector.tensor_copy(v_codes[0][:], tab[0][:].bitcast(U32).indirect(list1[:]))
-        nc.vector.tensor_copy(v_sc[:], tab_sc[:].indirect(list1[:]))
 
         w1_q = {}
 
@@ -165,7 +170,7 @@ def tile_list_slot_bidding_kernel(
                     lhsT=w1_q[index, a][0].bitcast(FP8X4),
                     lhsT_scale=w1_q[index, a][1],
                     rhs=v_codes[a][:, cols].bitcast(FP8X4),
-                    rhs_scale=v_sc[4 * a :, cols],
+                    rhs_scale=v_sc[:, a, cols],
                     start=(a == 0),
                     stop=(a == 1),
                 )

@@ -100,12 +100,17 @@ def tile_list_slot_bidding_kernel(
         nc.vector.memset(v_sc[:].rearrange("p a c -> p (a c)").bitcast(I32), 0)
         nc.vector.memset(wb_sc[:].rearrange("p a c -> p (a c)").bitcast(I32), 0)
         nc.sync.dma_start(list1[:], offs)
+        nc.sync.dma_start(list2[:], offs2)
         nc.sync.dma_start(out=tab[0][:], in_=tab_words[0].rearrange("p t i -> p (t i)").bitcast(I32))
         w1_a = load_w1("w1_a", 0, P)
         nc.sync.dma_start(out=tab[1][:], in_=tab_words[1].rearrange("p t i -> p (t i)").bitcast(I32))
-        nc.sync.dma_start(list2[:], offs2)
-        nc.sync.dma_start(out=wgs_rows[:, 0:BANK], in_=wgs[:, 0:BANK])
         load_page(0)
+        nc.sync.dma_start(out=wgs_rows[:, 0:BANK], in_=wgs[:, 0:BANK])
+        nc.vector.tensor_copy(picked_sc[:], tab_sc[:].indirect(list1[:]))
+        for q in range(QUADS):
+            nc.scalar.dma_start(
+                out=v_sc[32 * q : 32 * q + 4, :, :].bitcast(I32), in_=picked_sc[8 * q : 8 * q + 8, :].bitcast(I32)
+            )
         w1_b = load_w1("w1_b", P, 2 * P)
         nc.sync.dma_start(out=wgs_rows[:, BANK:], in_=wgs[:, BANK:])
         nc.sync.dma_start(list3[:], offs3)
@@ -122,11 +127,6 @@ def tile_list_slot_bidding_kernel(
         load_page(4)
         load_page(5)
 
-        nc.vector.tensor_copy(picked_sc[:], tab_sc[:].indirect(list1[:]))
-        for q in range(QUADS):
-            nc.gpsimd.dma_start(
-                out=v_sc[32 * q : 32 * q + 4, :, :].bitcast(I32), in_=picked_sc[8 * q : 8 * q + 8, :].bitcast(I32)
-            )
         v_codes = [own("v_codes0", [P, S], U32)]
         nc.vector.tensor_copy(v_codes[0][:], tab[0][:].bitcast(U32).indirect(list1[:]))
 

@@ -70,15 +70,15 @@ def tile_list_slot_bidding_kernel(
                 rows = page0[K_PASS:, :].rearrange("(p i) t -> i p t", i=PACK)[index - 4]
             nc.sync.dma_start(out=pages[index][:], in_=rows)
 
-        def load(name, rows, kb):
+        def load(name, rows, kb, queue=nc.sync):
             raw = placed(name, list(rows.shape), F32, kb)
-            nc.sync.dma_start(out=raw[:], in_=rows)
+            queue.dma_start(out=raw[:], in_=rows)
             return raw
 
-        def load_w1(name, first, last):
+        def load_w1(name, first, last, queue=nc.sync):
             kb = W1_RAW + first // 32
             width_kb = (last - first) // 64
-            return [load(f"{name}{a}", pass_rows(w1, a)[:, :, first:last], kb + width_kb * a) for a in range(2)]
+            return [load(f"{name}{a}", pass_rows(w1, a)[:, :, first:last], kb + width_kb * a, queue) for a in range(2)]
 
         def quantize(name, grouped, width, kb=None):
             shape = [P, width // PACK]
@@ -101,8 +101,9 @@ def tile_list_slot_bidding_kernel(
         nc.vector.memset(wb_sc[:].rearrange("p a c -> p (a c)").bitcast(I32), 0)
         nc.sync.dma_start(list1[:], offs)
         nc.sync.dma_start(list2[:], offs2)
+        nc.sync.dma_start(list3[:], offs3)
         nc.sync.dma_start(out=tab[0][:], in_=tab_words[0].rearrange("p t i -> p (t i)").bitcast(I32))
-        w1_a = load_w1("w1_a", 0, P)
+        w1_a = load_w1("w1_a", 0, P, nc.scalar)
         nc.sync.dma_start(out=tab[1][:], in_=tab_words[1].rearrange("p t i -> p (t i)").bitcast(I32))
         load_page(0)
         nc.sync.dma_start(out=wgs_rows[:, 0:BANK], in_=wgs[:, 0:BANK])
@@ -113,7 +114,6 @@ def tile_list_slot_bidding_kernel(
             )
         w1_b = load_w1("w1_b", P, 2 * P)
         nc.sync.dma_start(out=wgs_rows[:, BANK:], in_=wgs[:, BANK:])
-        nc.sync.dma_start(list3[:], offs3)
         load_page(1)
         w1_c = load_w1("w1_c", 2 * P, K_PASS)
         load_page(2)

@@ -225,11 +225,11 @@ def tile_list_slot_bidding_kernel(
             nc.sync.dma_start(out=x_planes[32 * index : 32 * index + 32, :, :], in_=x_rows[:])
         load_page(7)
 
-        def scatter(t):
-            nc.vector.tensor_tensor(pages[4 + t][:].indirect(list2[:]), hs[4 + t][:], wgs_planes[:, t, :], MULT)
+        def scatter(t, h):
+            nc.vector.tensor_tensor(pages[4 + t][:].indirect(list2[:]), h, wgs_planes[:, t, :], MULT)
 
         for t in range(3):
-            scatter(t)
+            scatter(t, hs[4 + t][:])
 
         wp_grouped = placed("g_wp", [P, 2 * PACK * N], BF16, GROUPED)
         for a in range(2):
@@ -241,11 +241,13 @@ def tile_list_slot_bidding_kernel(
             zg_low.append(placed(f"zg_low{u}", [P, PACK * BANK], BF16, TAB + 4 * u))
             nc.scalar.activation(woven(zg_low[u][:]), planar(x_planes[:, :, u * BANK : (u + 1) * BANK]), RELU)
         z_low.append(quantize("z_low0", zg_low[0][:], PACK * BANK, H_TILES + 28))
-        make_h(7, TAB)
-        z_low.append(quantize("z_low1", zg_low[1][:], PACK * BANK))
+        late = placed("late", [P, 16 * CHUNK], BF16, X_PLANES)
+        front = late[:, : 8 * CHUNK].bitcast(F32)
+        for u in range(2):
+            h_half(7, u, front[:, u * BANK : (u + 1) * BANK])
 
         out_view = out.rearrange("(b p) m -> p b m", p=P)
-        x_late, zg_high, z_high, brands = {}, {}, {}, {}
+        zg_high, z_high, brands = {}, {}, {}
         brand_bank = (0, 4, 0, 0)
         perf_bank = (2, 6, 4, 2)
 
@@ -260,17 +262,16 @@ def tile_list_slot_bidding_kernel(
             codes, scales, base = z_operand(c, a)
             for e in range(2):
                 b = 2 * u + e
-                for part in range(CHUNK // P):
-                    cols = slice(base + part * P, base + (part + 1) * P)
-                    nc.tensor.matmul_mx(
-                        out=banks[brand_bank[c] + u][:, e * CHUNK + part * P : e * CHUNK + (part + 1) * P],
-                        lhsT=wb_codes[:, a, 2 * b * P : 2 * (b + 1) * P].bitcast(FP4X4),
-                        lhsT_scale=wb_sc[:, a, b * P : (b + 1) * P],
-                        rhs=codes[:, cols].bitcast(FP8X4),
-                        rhs_scale=scales[:, cols],
-                        start=(a == 0 and e == 0 and part == 0),
-                        stop=(a == 1 and e == 1 and part == CHUNK // P - 1),
-                    )
+                cols = slice(base, base + CHUNK)
+                nc.tensor.matmul_mx(
+                    out=banks[brand_bank[c] + u][:, e * CHUNK : (e + 1) * CHUNK],
+                    lhsT=wb_codes[:, a, 2 * b * P : 2 * (b + 1) * P].bitcast(FP4X4),
+                    lhsT_scale=wb_sc[:, a, b * P : (b + 1) * P],
+                    rhs=codes[:, cols].bitcast(FP8X4),
+                    rhs_scale=scales[:, cols],
+                    start=(a == 0 and e == 0),
+                    stop=(a == 1 and e == 1),
+                )
 
         def perf(c, a, u):
             codes, scales, base = z_operand(c, a)
@@ -293,17 +294,21 @@ def tile_list_slot_bidding_kernel(
                 for u in range(2):
                     product(c, a, u)
 
-        def gather(c, t):
-            if t == 0:
-                x_late[c] = placed(f"x_late{c}", [P, PACK, CHUNK], BF16, (X_PLANES, H_TILES + 28)[c % 2])
+        def planes_of(c):
+            first = (8, 8, 4, 8)[c] * CHUNK
+            both = late[:, first : first + 8 * CHUNK].rearrange("p (t s) -> p t s", t=PACK)
+            return both[:, :, c % 2 * CHUNK : (c % 2 + 1) * CHUNK]
+
+        def gather(c, t, count=1):
+            first = ((8, 9, 4, 9)[c] + 2 * t) * CHUNK
             nc.vector.tensor_copy(
-                x_late[c][:, t, :],
-                pages[4 + t][:].indirect(list3[:, c * CHUNK // 16 : (c + 1) * CHUNK // 16]),
+                late[:, first : first + count * CHUNK],
+                pages[4 + t][:].indirect(list3[:, c * CHUNK // 16 : (c + count) * CHUNK // 16]),
             )
 
         def rectify(c):
             zg_high[c] = placed(f"zg_high{c}", [P, PACK * CHUNK], BF16, GROUPED + 8 + 2 * c)
-            nc.scalar.activation(woven(zg_high[c][:]), planar(x_late[c][:]), RELU)
+            nc.scalar.activation(woven(zg_high[c][:]), planar(planes_of(c)), RELU)
 
         def quantize_chunk(c):
             z_high[c] = quantize(f"z_high{c}", zg_high[c][:], PACK * CHUNK)
@@ -314,7 +319,10 @@ def tile_list_slot_bidding_kernel(
                 nc.scalar.copy(out=brands[c][u][:], in_=banks[(perf_bank if c == 3 else brand_bank)[c] + u][:])
 
         def finish(c):
-            result = placed(f"result{c}", [P, 2, BANK], F32, (X_PLANES, H_TILES + 28, W1_RAW + 24, W1_RAW + 28)[c])
+            if c == 0:
+                result = front.rearrange("p (u m) -> p u m", u=2)
+            else:
+                result = placed(f"result{c}", [P, 2, BANK], F32, W1_RAW + (0, 16, 24, 28)[c])
             for u in range(2):
                 second = banks[(brand_bank if c == 3 else perf_bank)[c] + u]
                 nc.vector.tensor_tensor(result[:, u, :], second[:], brands[c][u][:], MAX)
@@ -326,39 +334,44 @@ def tile_list_slot_bidding_kernel(
         multiply(0, 0)
         multiply(1, 0)
         for t in range(3):
-            gather(0, t)
-        scatter(3)
-        gather(1, 0)
+            gather(0, t, 2)
+        scatter(3, front)
+        z_low.append(quantize("z_low1", zg_low[1][:], PACK * BANK, H_TILES + 28))
         gather(0, 3)
-        for t in range(1, PACK):
-            gather(1, t)
+        gather(1, 3)
+        gather(2, 0)
+        gather(2, 1)
         rectify(0)
         quantize_chunk(0)
         multiply(0, 1)
         rectify(1)
-        gather(2, 0)
-        gather(2, 1)
-        quantize_chunk(1)
-        multiply(1, 1)
         gather(2, 2)
         gather(2, 3)
+        quantize_chunk(1)
+        multiply(1, 1)
         copy_first(0)
         rectify(2)
-        for t in range(PACK):
-            gather(3, t)
-        copy_first(1)
-        multiply(2, 0)
+        gather(3, 0)
+        gather(3, 1)
         quantize_chunk(2)
-        multiply(2, 1)
-        finish(0)
-        rectify(3)
-        quantize_chunk(3)
-        copy_first(2)
-        for product in (perf, brand):
+        gather(3, 2)
+        gather(3, 3)
+        copy_first(1)
+        for product in (brand, perf):
             for a in range(2):
                 for u in range(2):
-                    product(3, a, u)
+                    product(2, a, u)
+        finish(0)
+        rectify(3)
         finish(1)
+        quantize_chunk(3)
+        copy_first(2)
+        for a in range(2):
+            for u in range(2):
+                perf(3, a, u)
+        for u in range(2):
+            for a in range(2):
+                brand(3, a, u)
         finish(2)
         copy_first(3)
         finish(3)

@@ -100,13 +100,13 @@ def tile_list_slot_bidding_kernel(
         nc.vector.memset(v_sc[:].rearrange("p a c -> p (a c)").bitcast(I32), 0)
         nc.vector.memset(wb_sc[:].rearrange("p a c -> p (a c)").bitcast(I32), 0)
         nc.sync.dma_start(list1[:], offs)
-        nc.sync.dma_start(list2[:], offs2)
-        nc.sync.dma_start(list3[:], offs3)
         nc.sync.dma_start(out=tab[0][:], in_=tab_words[0].rearrange("p t i -> p (t i)").bitcast(I32))
         w1_a = load_w1("w1_a", 0, P, nc.scalar)
         nc.sync.dma_start(out=tab[1][:], in_=tab_words[1].rearrange("p t i -> p (t i)").bitcast(I32))
+        nc.sync.dma_start(out=wgs_rows[:, 0:CHUNK], in_=wgs[:, 0:CHUNK])
+        nc.sync.dma_start(list2[:], offs2)
         load_page(0)
-        nc.sync.dma_start(out=wgs_rows[:, 0:BANK], in_=wgs[:, 0:BANK])
+        nc.sync.dma_start(out=wgs_rows[:, CHUNK:BANK], in_=wgs[:, CHUNK:BANK])
         nc.vector.tensor_copy(picked_sc[:], tab_sc[:].indirect(list1[:]))
         for q in range(QUADS):
             nc.scalar.dma_start(
@@ -114,6 +114,7 @@ def tile_list_slot_bidding_kernel(
             )
         w1_b = load_w1("w1_b", P, 2 * P)
         nc.sync.dma_start(out=wgs_rows[:, BANK:], in_=wgs[:, BANK:])
+        nc.sync.dma_start(list3[:], offs3)
         load_page(1)
         w1_c = load_w1("w1_c", 2 * P, K_PASS)
         load_page(2)
@@ -146,10 +147,11 @@ def tile_list_slot_bidding_kernel(
         quantize_w1("w1_a", w1_a, 0, 1)
 
         v_codes.append(placed("v_codes1", [P, S], U32, TAB_SC))
-        for u in range(2):
+        pieces = ((0, CHUNK), (CHUNK, BANK), (BANK, S))
+        for first, last in pieces:
             nc.vector.tensor_copy(
-                v_codes[1][:, u * BANK : (u + 1) * BANK],
-                tab[1][:].bitcast(U32).indirect(list1[:, u * 32 : (u + 1) * 32]),
+                v_codes[1][:, first:last],
+                tab[1][:].bitcast(U32).indirect(list1[:, first // 16 : last // 16]),
             )
 
         load_page(6)
@@ -161,12 +163,10 @@ def tile_list_slot_bidding_kernel(
                 in_=wb_scales[:, 4 * q : 4 * q + 4, :].rearrange("a r c -> r a c").bitcast(I32),
             )
 
-        def h_half(index, u, dest):
-            cols = slice(u * BANK, (u + 1) * BANK)
-            bank = banks[(2 * index + u) % 8]
+        def h_part(index, cols, bank, dest):
             for a in range(2):
                 nc.tensor.matmul_mx(
-                    out=bank[:],
+                    out=bank,
                     lhsT=w1_q[index, a][0].bitcast(FP8X4),
                     lhsT_scale=w1_q[index, a][1],
                     rhs=v_codes[a][:, cols].bitcast(FP8X4),
@@ -174,7 +174,10 @@ def tile_list_slot_bidding_kernel(
                     start=(a == 0),
                     stop=(a == 1),
                 )
-            nc.scalar.copy(out=dest, in_=bank[:])
+            nc.scalar.copy(out=dest, in_=bank)
+
+        def h_half(index, u, dest):
+            h_part(index, slice(u * BANK, (u + 1) * BANK), banks[(2 * index + u) % 8][:], dest)
 
         hs = {}
 
@@ -183,16 +186,13 @@ def tile_list_slot_bidding_kernel(
             for u in range(2):
                 h_half(index, u, hs[index][:, u * BANK : (u + 1) * BANK])
 
-        for u in range(2):
-            if u == 1:
+        for n, (first, last) in enumerate(pieces):
+            if n == 2:
                 quantize_w1("w1_b", w1_b, 1, 1)
-            half = placed(f"h0_{u}", [P, BANK], F32, (H_TILES, W1_RAW + 6)[u])
-            h_half(0, u, half[:])
+            part = placed(f"h0_{n}", [P, last - first], F32, (H_TILES, H_TILES + 1, W1_RAW + 6)[n])
+            h_part(0, slice(first, last), banks[(0, 1, 7)[n]][:, : last - first], part[:])
             nc.vector.tensor_tensor(
-                pages[0][:].indirect(list2[:, u * 32 : (u + 1) * 32]),
-                half[:],
-                wgs_rows[:, u * BANK : (u + 1) * BANK],
-                MULT,
+                pages[0][:].indirect(list2[:, first // 16 : last // 16]), part[:], wgs_rows[:, first:last], MULT
             )
 
         make_h(1)

@@ -236,11 +236,12 @@ def tile_list_slot_bidding_kernel(
             nc.scalar.copy(out=woven(wp_grouped[:, a * PACK * N : (a + 1) * PACK * N]), in_=planar(wp_raw[a][:]))
         wp_codes, wp_sc = quantize("wp", wp_grouped[:], 2 * PACK * N)
 
-        zg_low, z_low = [], []
-        for u in range(2):
-            zg_low.append(placed(f"zg_low{u}", [P, PACK * BANK], BF16, TAB + 4 * u))
-            nc.scalar.activation(woven(zg_low[u][:]), planar(x_planes[:, :, u * BANK : (u + 1) * BANK]), RELU)
-        z_low.append(quantize("z_low0", zg_low[0][:], PACK * BANK, H_TILES + 28))
+        zg_low, z_low = {}, {}
+        for c, count in ((1, 2), (3, 1), (0, 1)):
+            zg_low[c] = placed(f"zg_low{c}", [P, PACK * count * CHUNK], BF16, TAB + 2 * c)
+            nc.scalar.activation(woven(zg_low[c][:]), planar(x_planes[:, :, c * CHUNK : (c + count) * CHUNK]), RELU)
+        z_low[3] = quantize("z_low3", zg_low[3][:], PACK * CHUNK) + (0,)
+        z_low[0] = quantize("z_low0", zg_low[0][:], PACK * CHUNK, H_TILES + 28) + (0,)
         late = placed("late", [P, 16 * CHUNK], BF16, X_PLANES)
         front = late[:, : 8 * CHUNK].bitcast(F32)
         for u in range(2):
@@ -253,8 +254,7 @@ def tile_list_slot_bidding_kernel(
 
         def z_operand(c, a):
             if a == 0:
-                codes, scales = z_low[c * CHUNK // BANK]
-                return codes, scales, c * CHUNK % BANK
+                return z_low[c]
             codes, scales = z_high[c]
             return codes, scales, 0
 
@@ -295,14 +295,17 @@ def tile_list_slot_bidding_kernel(
                     product(c, a, u)
 
         def planes_of(c):
-            first = (8, 8, 4, 8)[c] * CHUNK
-            both = late[:, first : first + 8 * CHUNK].rearrange("p (t s) -> p t s", t=PACK)
+            if c == 3:
+                return last[:]
+            if c == 2:
+                return late[:, 6 * CHUNK : 10 * CHUNK].rearrange("p (t s) -> p t s", t=PACK)
+            both = late[:, 8 * CHUNK :].rearrange("p (t s) -> p t s", t=PACK)
             return both[:, :, c % 2 * CHUNK : (c % 2 + 1) * CHUNK]
 
         def gather(c, t, count=1):
-            first = ((8, 9, 4, 9)[c] + 2 * t) * CHUNK
+            first = (6 + t if c == 2 else 8 + c % 2 + 2 * t) * CHUNK
             nc.vector.tensor_copy(
-                late[:, first : first + count * CHUNK],
+                last[:, t, :] if c == 3 else late[:, first : first + count * CHUNK],
                 pages[4 + t][:].indirect(list3[:, c * CHUNK // 16 : (c + count) * CHUNK // 16]),
             )
 
@@ -311,7 +314,7 @@ def tile_list_slot_bidding_kernel(
             nc.scalar.activation(woven(zg_high[c][:]), planar(planes_of(c)), RELU)
 
         def quantize_chunk(c):
-            z_high[c] = quantize(f"z_high{c}", zg_high[c][:], PACK * CHUNK)
+            z_high[c] = quantize(f"z_high{c}", zg_high[c][:], PACK * CHUNK, GROUPED + 12 if c == 1 else None)
 
         def copy_first(c):
             brands[c] = [placed(f"first{c}_{u}", [P, BANK], F32, W1_RAW + 4 * c + 2 * u) for u in range(2)]
@@ -322,7 +325,7 @@ def tile_list_slot_bidding_kernel(
             if c == 0:
                 result = front.rearrange("p (u m) -> p u m", u=2)
             else:
-                result = placed(f"result{c}", [P, 2, BANK], F32, W1_RAW + (0, 16, 24, 28)[c])
+                result = placed(f"result{c}", [P, 2, BANK], F32, (0, GROUPED + 8, W1_RAW + 24, W1_RAW + 28)[c])
             for u in range(2):
                 second = banks[(brand_bank if c == 3 else perf_bank)[c] + u]
                 nc.vector.tensor_tensor(result[:, u, :], second[:], brands[c][u][:], MAX)
@@ -332,11 +335,12 @@ def tile_list_slot_bidding_kernel(
                 )
 
         multiply(0, 0)
-        multiply(1, 0)
         for t in range(3):
             gather(0, t, 2)
         scatter(3, front)
-        z_low.append(quantize("z_low1", zg_low[1][:], PACK * BANK, H_TILES + 28))
+        middle = quantize("z_low1", zg_low[1][:], PACK * BANK, H_TILES + 28)
+        z_low[1], z_low[2] = middle + (0,), middle + (CHUNK,)
+        multiply(1, 0)
         gather(0, 3)
         gather(1, 3)
         gather(2, 0)
@@ -344,27 +348,24 @@ def tile_list_slot_bidding_kernel(
         rectify(0)
         quantize_chunk(0)
         multiply(0, 1)
-        rectify(1)
         gather(2, 2)
-        gather(2, 3)
+        rectify(1)
         quantize_chunk(1)
+        gather(2, 3)
         multiply(1, 1)
         copy_first(0)
-        rectify(2)
-        gather(3, 0)
-        gather(3, 1)
-        quantize_chunk(2)
-        gather(3, 2)
-        gather(3, 3)
+        last = placed("last", [P, PACK, CHUNK], BF16, GROUPED + 10)
+        for t in range(PACK):
+            gather(3, t)
         copy_first(1)
-        for product in (brand, perf):
-            for a in range(2):
-                for u in range(2):
-                    product(2, a, u)
+        rectify(2)
+        quantize_chunk(2)
+        multiply(2, 0)
+        multiply(2, 1)
         finish(0)
         rectify(3)
-        finish(1)
         quantize_chunk(3)
+        finish(1)
         copy_first(2)
         for a in range(2):
             for u in range(2):

@@ -23,6 +23,7 @@ K_PASS = P * PACK
 BANK = 512
 CHUNK = 256
 QUADS = 4
+TAIL = 64
 KB = 1024
 
 TAB, TAB_SC, PAGES, W1_RAW, PLANES, H_TILES, GROUPED, X_PLANES = 0, 32, 36, 84, 116, 132, 164, 180
@@ -112,7 +113,10 @@ def tile_list_slot_bidding_kernel(
             nc.scalar.dma_start(
                 out=v_sc[32 * q : 32 * q + 4, :, :].bitcast(I32), in_=picked_sc[8 * q : 8 * q + 8, :].bitcast(I32)
             )
-        w1_b = load_w1("w1_b", P, 2 * P)
+        w1_b = [load("w1_b0", pass_rows(w1, 0)[:, :, P : 2 * P], W1_RAW + 4)]
+        h0_last = own("h0_last", [P, 2 * BANK - TAIL], F32)
+        w1_b.append(h0_last[:, BANK - TAIL :].rearrange("p (j c) -> p j c", j=PACK))
+        nc.sync.dma_start(out=w1_b[1], in_=pass_rows(w1, 1)[:, :, P : 2 * P])
         nc.sync.dma_start(out=wgs_rows[:, BANK:], in_=wgs[:, BANK:])
         nc.sync.dma_start(list3[:], offs3)
         load_page(1)
@@ -163,7 +167,7 @@ def tile_list_slot_bidding_kernel(
                 in_=wb_scales[:, 4 * q : 4 * q + 4, :].rearrange("a r c -> r a c").bitcast(I32),
             )
 
-        def h_part(index, cols, bank, dest):
+        def h_part(index, cols, bank, dest, split=None):
             for a in range(2):
                 nc.tensor.matmul_mx(
                     out=bank,
@@ -174,7 +178,11 @@ def tile_list_slot_bidding_kernel(
                     start=(a == 0),
                     stop=(a == 1),
                 )
-            nc.scalar.copy(out=dest, in_=bank)
+            if split is None:
+                nc.scalar.copy(out=dest, in_=bank)
+            else:
+                nc.scalar.copy(out=dest[:, :split], in_=bank[:, :split])
+                nc.scalar.copy(out=dest[:, split:], in_=bank[:, split:])
 
         def h_half(index, u, dest):
             h_part(index, slice(u * BANK, (u + 1) * BANK), banks[(2 * index + u) % 8][:], dest)
@@ -189,8 +197,11 @@ def tile_list_slot_bidding_kernel(
         for n, (first, last) in enumerate(pieces):
             if n == 2:
                 quantize_w1("w1_b", w1_b, 1, 1)
-            part = placed(f"h0_{n}", [P, last - first], F32, (H_TILES, H_TILES + 1, W1_RAW + 6)[n])
-            h_part(0, slice(first, last), banks[(0, 1, 7)[n]][:, : last - first], part[:])
+                part = h0_last[:, :BANK]
+                h_part(0, slice(first, last), banks[7][:], part, BANK - TAIL)
+            else:
+                part = placed(f"h0_{n}", [P, last - first], F32, H_TILES + n)
+                h_part(0, slice(first, last), banks[n][:, : last - first], part[:])
             nc.vector.tensor_tensor(
                 pages[0][:].indirect(list2[:, first // 16 : last // 16]), part[:], wgs_rows[:, first:last], MULT
             )

@@ -28,6 +28,8 @@ KB = 1024
 
 TAB, TAB_SC, PAGES, W1_RAW, PLANES, H_TILES, GROUPED, X_PLANES = 0, 32, 36, 84, 116, 132, 164, 180
 
+CHUNK_START = (0, CHUNK, 2 * CHUNK, 3 * CHUNK)
+
 
 def tile_list_slot_bidding_kernel(
     tc, tab_words, tab_scales, offs, offs2, offs3, w1, wgs, page0, wb_words, wb_scales, wp, out
@@ -44,32 +46,19 @@ def tile_list_slot_bidding_kernel(
             return keep.tile(shape, dtype, name=name, align_bytes=64)
 
         def placed(name, shape, dtype, kb):
-            return shared.tile(shape, dtype, name=name, align_bytes=64, offset=kb * KB)
+            return shared.tile(shape, dtype, name=name, align_bytes=64, offset=int(kb * KB))
 
-        list1 = lists.tile([P, S // 16], U16, name="list1")
-        list2 = lists.tile([P, S // 16], U16, name="list2")
-        list3 = lists.tile([P, SLOTS // 16], U16, name="list3")
-        tab = [placed(f"tab{a}", [P, T], I32, TAB + 16 * a) for a in range(2)]
-        tab_sc = placed("tab_sc", [P, T], U8, TAB_SC)
-        picked_sc = own("picked_sc", [P, S], U8)
-        v_sc = own("v_sc", [P, 2, S], U8)
-        wb_codes = own("wb_codes", [P, 2, 2 * N], U8)
-        wb_sc = own("wb_sc", [P, 2, N], U8)
-        wgs_rows = own("wgs_rows", [P, S], F32)
+        def entries(index_list, first, count):
+            return index_list[:, first // 16 : (first + count) // 16]
 
         def pass_rows(w, a):
             return w[a * K_PASS : (a + 1) * K_PASS, :].rearrange("(p j) c -> p j c", j=PACK)
 
-        pages = {}
+        def woven(flat):
+            return flat.rearrange("p (c i j) -> p c j i", i=4, j=PACK)
 
-        def load_page(index):
-            kb = PAGES + 8 * index if index < 6 else TAB + 16 + 8 * (index - 6)
-            pages[index] = placed(f"page{index}", [P, T2], F32, kb)
-            if index < 4:
-                rows = page0[index * P : (index + 1) * P, :]
-            else:
-                rows = page0[K_PASS:, :].rearrange("(p i) t -> i p t", i=PACK)[index - 4]
-            nc.sync.dma_start(out=pages[index][:], in_=rows)
+        def planar(planes):
+            return planes.rearrange("p j (c i) -> p c j i", i=4)
 
         def load(name, rows, kb, queue=nc.sync):
             raw = placed(name, list(rows.shape), F32, kb)
@@ -81,6 +70,16 @@ def tile_list_slot_bidding_kernel(
             width_kb = (last - first) // 64
             return [load(f"{name}{a}", pass_rows(w1, a)[:, :, first:last], kb + width_kb * a, queue) for a in range(2)]
 
+        pages = {}
+
+        def load_page(index):
+            kb = PAGES + 8 * index if index < 6 else TAB + 16 + 8 * (index - 6)
+            if index < 4:
+                rows = page0[index * P : (index + 1) * P, :]
+            else:
+                rows = page0[K_PASS:, :].rearrange("(p i) t -> i p t", i=PACK)[index - 4]
+            pages[index] = load(f"page{index}", rows, kb)
+
         def quantize(name, grouped, width, kb=None):
             shape = [P, width // PACK]
             codes = own(name + "_codes", shape, U32) if kb is None else placed(name + "_codes", shape, U32, kb)
@@ -88,11 +87,16 @@ def tile_list_slot_bidding_kernel(
             nc.vector.quantize_mx(out=codes[:].bitcast(FP8X4), scales=scales[:], in_=grouped)
             return codes, scales
 
-        def woven(flat):
-            return flat.rearrange("p (c i j) -> p c j i", i=4, j=PACK)
-
-        def planar(planes):
-            return planes.rearrange("p j (c i) -> p c j i", i=4)
+        list1 = lists.tile([P, S // 16], U16, name="list1")
+        list2 = lists.tile([P, S // 16], U16, name="list2")
+        list3 = lists.tile([P, SLOTS // 16], U16, name="list3")
+        tab = [placed(f"tab{a}", [P, T], I32, TAB + 16 * a) for a in range(2)]
+        tab_sc = placed("tab_sc", [P, T], U8, TAB_SC)
+        picked_sc = own("picked_sc", [P, S], U8)
+        v_sc = own("v_sc", [P, 2, S], U8)
+        wb_codes = own("wb_codes", [P, 2, 2 * N], U8)
+        wb_sc = own("wb_sc", [P, 2, N], U8)
+        wgs_rows = own("wgs_rows", [P, S], F32)
 
         for a in range(2):
             nc.sync.dma_start(out=tab_sc[a:32:2, :].bitcast(I32), in_=tab_scales[a].bitcast(I32))
@@ -154,8 +158,7 @@ def tile_list_slot_bidding_kernel(
         pieces = ((0, CHUNK), (CHUNK, BANK), (BANK, S))
         for first, last in pieces:
             nc.vector.tensor_copy(
-                v_codes[1][:, first:last],
-                tab[1][:].bitcast(U32).indirect(list1[:, first // 16 : last // 16]),
+                v_codes[1][:, first:last], tab[1][:].bitcast(U32).indirect(entries(list1, first, last - first))
             )
 
         load_page(6)
@@ -184,15 +187,16 @@ def tile_list_slot_bidding_kernel(
                 nc.scalar.copy(out=dest[:, :split], in_=bank[:, :split])
                 nc.scalar.copy(out=dest[:, split:], in_=bank[:, split:])
 
-        def h_half(index, u, dest):
-            h_part(index, slice(u * BANK, (u + 1) * BANK), banks[(2 * index + u) % 8][:], dest)
+        def make_h(index, dest, first_bank):
+            for u in range(2):
+                cols = slice(u * BANK, (u + 1) * BANK)
+                h_part(index, cols, banks[first_bank + u][:], dest[:, cols])
 
         hs = {}
 
-        def make_h(index, kb=None):
-            hs[index] = placed(f"h{index}", [P, S], F32, H_TILES + 4 * index if kb is None else kb)
-            for u in range(2):
-                h_half(index, u, hs[index][:, u * BANK : (u + 1) * BANK])
+        def make_h_tile(index):
+            hs[index] = placed(f"h{index}", [P, S], F32, H_TILES + 4 * index)
+            make_h(index, hs[index], 2 * index % 8)
 
         for n, (first, last) in enumerate(pieces):
             if n == 2:
@@ -200,16 +204,16 @@ def tile_list_slot_bidding_kernel(
                 part = h0_last[:, :BANK]
                 h_part(0, slice(first, last), banks[7][:], part, BANK - TAIL)
             else:
-                part = placed(f"h0_{n}", [P, last - first], F32, H_TILES + n)
-                h_part(0, slice(first, last), banks[n][:, : last - first], part[:])
+                part = placed(f"h0_{n}", [P, last - first], F32, H_TILES + n)[:]
+                h_part(0, slice(first, last), banks[n][:, : last - first], part)
             nc.vector.tensor_tensor(
-                pages[0][:].indirect(list2[:, first // 16 : last // 16]), part[:], wgs_rows[:, first:last], MULT
+                pages[0][:].indirect(entries(list2, first, last - first)), part, wgs_rows[:, first:last], MULT
             )
 
-        make_h(1)
+        make_h_tile(1)
         quantize_w1("w1_c", w1_c, 2, 2)
-        make_h(2)
-        make_h(3)
+        make_h_tile(2)
+        make_h_tile(3)
 
         grouped = placed("g_w1_d", [P, 2 * PACK * K_PASS], BF16, GROUPED + 8)
         for a in range(2):
@@ -225,7 +229,7 @@ def tile_list_slot_bidding_kernel(
                 cols = slice(a * K_PASS + t * P, a * K_PASS + (t + 1) * P)
                 w1_q[4 + t, a] = (codes[:, cols], scales[:, cols])
         for index in range(4, 7):
-            make_h(index)
+            make_h_tile(index)
 
         x_planes = placed("x_planes", [P, PACK, SLOTS], BF16, X_PLANES)
         for index in range(4):
@@ -247,143 +251,148 @@ def tile_list_slot_bidding_kernel(
             nc.scalar.copy(out=woven(wp_grouped[:, a * PACK * N : (a + 1) * PACK * N]), in_=planar(wp_raw[a][:]))
         wp_codes, wp_sc = quantize("wp", wp_grouped[:], 2 * PACK * N)
 
-        zg_low, z_low = {}, {}
-        for c, count in ((1, 2), (3, 1), (0, 1)):
-            zg_low[c] = placed(f"zg_low{c}", [P, PACK * count * CHUNK], BF16, TAB + 2 * c)
-            nc.scalar.activation(woven(zg_low[c][:]), planar(x_planes[:, :, c * CHUNK : (c + count) * CHUNK]), RELU)
-        z_low[3] = quantize("z_low3", zg_low[3][:], PACK * CHUNK) + (0,)
-        z_low[0] = quantize("z_low0", zg_low[0][:], PACK * CHUNK, H_TILES + 28) + (0,)
-        late = placed("late", [P, 16 * CHUNK], BF16, X_PLANES)
-        front = late[:, : 8 * CHUNK].bitcast(F32)
-        for u in range(2):
-            h_half(7, u, front[:, u * BANK : (u + 1) * BANK])
+        WORDS = PACK * CHUNK
+
+        def rectify(dest, planes):
+            nc.scalar.activation(woven(dest), planar(planes), RELU)
+
+        low_0 = placed("low_0", [P, WORDS], BF16, TAB)
+        low_12 = placed("low_12", [P, 2 * WORDS], BF16, TAB + 2)
+        high0_low3 = placed("high0_low3", [P, 2 * WORDS], BF16, TAB + 8)
+        rectify(low_12[:], x_planes[:, :, CHUNK : 3 * CHUNK])
+        rectify(high0_low3[:, WORDS:], x_planes[:, :, 3 * CHUNK :])
+        rectify(low_0[:], x_planes[:, :, :CHUNK])
+        z = {(0, 0): quantize("z_low0", low_0[:], WORDS, H_TILES + 28) + (0,)}
+
+        late = placed("late", [P, 25 * CHUNK], BF16, X_PLANES)
+
+        def runs(first, pitch, count, width):
+            lead = min(first, pitch - width)
+            start = int((first - lead) * CHUNK)
+            whole = late[:, start : start + int(count * pitch * CHUNK)].rearrange("p (r s) -> p r s", r=count)
+            return whole[:, :, int(lead * CHUNK) : int((lead + width) * CHUNK)]
+
+        h7 = runs(0, 8, 1, 8)[:, 0, :].bitcast(F32)
+        make_h(7, h7, 2)
+        plane_places = ((8, 1), (12.5, 3.75), (4, 4), (5, 6))
+
+        def planes_of(c):
+            return runs(plane_places[c][0], plane_places[c][1], PACK, 1)
+
+        def plane_pair(c0, c1, t):
+            first, second = (plane_places[c][0] + t * plane_places[c][1] for c in (c0, c1))
+            return runs(first, second - first, 2, 1)
 
         out_view = out.rearrange("(b p) m -> p b m", p=P)
-        zg_high, z_high, brands = {}, {}, {}
-        brand_bank = (0, 4, 0, 0)
-        perf_bank = (2, 6, 4, 2)
+        brand_banks = ((0, 1), (4, 5), (0, 1), (6, 0))
+        perf_banks = ((2, 3), (6, 7), (4, 5), (2, 3))
 
-        def z_operand(c, a):
-            if a == 0:
-                return z_low[c]
-            codes, scales = z_high[c]
-            return codes, scales, 0
+        def passes(c, a, u, bank, weights):
+            codes, scales, base = z[c, a]
+            cols = slice(base, base + CHUNK)
+            for e in range(2):
+                w_codes, w_scales = weights(a, 2 * u + e)
+                nc.tensor.matmul_mx(
+                    out=banks[bank][:, e * CHUNK : (e + 1) * CHUNK],
+                    lhsT=w_codes,
+                    lhsT_scale=w_scales,
+                    rhs=codes[:, cols].bitcast(FP8X4),
+                    rhs_scale=scales[:, cols],
+                    start=(a == 0 and e == 0),
+                    stop=(a == 1 and e == 1),
+                )
+
+        def brand_weights(a, b):
+            return wb_codes[:, a, 2 * b * P : 2 * (b + 1) * P].bitcast(FP4X4), wb_sc[:, a, b * P : (b + 1) * P]
+
+        def perf_weights(a, b):
+            cols = slice(a * N + b * P, a * N + (b + 1) * P)
+            return wp_codes[:, cols].bitcast(FP8X4), wp_sc[:, cols]
 
         def brand(c, a, u):
-            codes, scales, base = z_operand(c, a)
-            for e in range(2):
-                b = 2 * u + e
-                cols = slice(base, base + CHUNK)
-                nc.tensor.matmul_mx(
-                    out=banks[brand_bank[c] + u][:, e * CHUNK : (e + 1) * CHUNK],
-                    lhsT=wb_codes[:, a, 2 * b * P : 2 * (b + 1) * P].bitcast(FP4X4),
-                    lhsT_scale=wb_sc[:, a, b * P : (b + 1) * P],
-                    rhs=codes[:, cols].bitcast(FP8X4),
-                    rhs_scale=scales[:, cols],
-                    start=(a == 0 and e == 0),
-                    stop=(a == 1 and e == 1),
-                )
+            passes(c, a, u, brand_banks[c][u], brand_weights)
 
         def perf(c, a, u):
-            codes, scales, base = z_operand(c, a)
-            for e in range(2):
-                b = 2 * u + e
-                cols = slice(base, base + CHUNK)
-                w_cols = slice(a * N + b * P, a * N + (b + 1) * P)
-                nc.tensor.matmul_mx(
-                    out=banks[perf_bank[c] + u][:, e * CHUNK : (e + 1) * CHUNK],
-                    lhsT=wp_codes[:, w_cols].bitcast(FP8X4),
-                    lhsT_scale=wp_sc[:, w_cols],
-                    rhs=codes[:, cols].bitcast(FP8X4),
-                    rhs_scale=scales[:, cols],
-                    start=(a == 0 and e == 0),
-                    stop=(a == 1 and e == 1),
-                )
+            passes(c, a, u, perf_banks[c][u], perf_weights)
 
         def multiply(c, a):
             for product in (brand, perf):
                 for u in range(2):
                     product(c, a, u)
 
-        def planes_of(c):
-            if c == 3:
-                return last[:]
-            if c == 2:
-                return late[:, 6 * CHUNK : 10 * CHUNK].rearrange("p (t s) -> p t s", t=PACK)
-            both = late[:, 8 * CHUNK :].rearrange("p (t s) -> p t s", t=PACK)
-            return both[:, :, c % 2 * CHUNK : (c % 2 + 1) * CHUNK]
+        def gather(dest, t, first, count):
+            nc.vector.tensor_copy(dest, pages[4 + t][:].indirect(entries(list3, first, count)))
 
-        def gather(c, t, count=1):
-            first = (6 + t if c == 2 else 8 + c % 2 + 2 * t) * CHUNK
-            nc.vector.tensor_copy(
-                last[:, t, :] if c == 3 else late[:, first : first + count * CHUNK],
-                pages[4 + t][:].indirect(list3[:, c * CHUNK // 16 : (c + count) * CHUNK // 16]),
+        copied = {}
+
+        def copy_out(c, u):
+            copied[c, u] = placed(f"copied{c}_{u}", [P, BANK], F32, W1_RAW + 4 * c + 2 * u)
+            nc.scalar.copy(out=copied[c, u][:], in_=banks[(perf_banks if c == 3 else brand_banks)[c][u]][:])
+
+        def finish(c, u, result=None, kb=None):
+            if result is None:
+                own_result = placed(f"result{c}_{u}", [P, BANK], F32, kb or W1_RAW + 16 + 4 * c + 2 * u)
+                result = own_result[:].rearrange("p (e m) -> p e m", e=2)
+            other = banks[(brand_banks if c == 3 else perf_banks)[c][u]]
+            nc.vector.tensor_tensor(
+                result,
+                other[:].rearrange("p (e m) -> p e m", e=2),
+                copied[c, u][:].rearrange("p (e m) -> p e m", e=2),
+                MAX,
             )
+            nc.sync.dma_start(out=out_view[:, 2 * u : 2 * u + 2, CHUNK_START[c] : CHUNK_START[c] + CHUNK], in_=result)
 
-        def rectify(c):
-            zg_high[c] = placed(f"zg_high{c}", [P, PACK * CHUNK], BF16, GROUPED + 8 + 2 * c)
-            nc.scalar.activation(woven(zg_high[c][:]), planar(planes_of(c)), RELU)
-
-        def quantize_chunk(c):
-            z_high[c] = quantize(f"z_high{c}", zg_high[c][:], PACK * CHUNK, GROUPED + 12 if c == 1 else None)
-
-        def copy_first(c):
-            brands[c] = [placed(f"first{c}_{u}", [P, BANK], F32, W1_RAW + 4 * c + 2 * u) for u in range(2)]
-            for u in range(2):
-                nc.scalar.copy(out=brands[c][u][:], in_=banks[(perf_bank if c == 3 else brand_bank)[c] + u][:])
-
-        def finish(c):
-            if c == 0:
-                result = front.rearrange("p (u m) -> p u m", u=2)
-            else:
-                result = placed(f"result{c}", [P, 2, BANK], F32, (0, GROUPED + 8, W1_RAW + 24, W1_RAW + 28)[c])
-            for u in range(2):
-                second = banks[(brand_bank if c == 3 else perf_bank)[c] + u]
-                nc.vector.tensor_tensor(result[:, u, :], second[:], brands[c][u][:], MAX)
-                nc.sync.dma_start(
-                    out=out_view[:, 2 * u : 2 * u + 2, c * CHUNK : (c + 1) * CHUNK],
-                    in_=result[:, u, :].rearrange("p (e m) -> p e m", e=2),
-                )
+        def in_late(first):
+            return runs(first, 2, 2, 2).bitcast(F32)
 
         multiply(0, 0)
         for t in range(3):
-            gather(0, t, 2)
-        scatter(3, front)
-        middle = quantize("z_low1", zg_low[1][:], PACK * BANK, H_TILES + 28)
-        z_low[1], z_low[2] = middle + (0,), middle + (CHUNK,)
+            gather(plane_pair(0, 1, t), t, 0, 2 * CHUNK)
+        scatter(3, h7)
+        middle = quantize("z_low12", low_12[:], 2 * WORDS, H_TILES + 28)
+        z[1, 0], z[2, 0] = middle + (0,), middle + (CHUNK,)
         multiply(1, 0)
-        gather(0, 3)
-        gather(1, 3)
-        gather(2, 0)
-        gather(2, 1)
-        rectify(0)
-        quantize_chunk(0)
+        for c in (0, 1):
+            gather(planes_of(c)[:, 3, :], 3, CHUNK_START[c], CHUNK)
+        gather(plane_pair(2, 3, 0), 0, 2 * CHUNK, 2 * CHUNK)
+        rectify(high0_low3[:, :WORDS], planes_of(0))
+        both = quantize("z_high0", high0_low3[:], 2 * WORDS)
+        z[0, 1], z[3, 0] = both + (0,), both + (CHUNK,)
         multiply(0, 1)
-        gather(2, 2)
-        rectify(1)
-        quantize_chunk(1)
-        gather(2, 3)
+        gather(plane_pair(2, 3, 1), 1, 2 * CHUNK, 2 * CHUNK)
+        high = {1: placed("high1", [P, WORDS], BF16, GROUPED + 8)}
+        rectify(high[1][:], planes_of(1))
+        z[1, 1] = quantize("z_high1", high[1][:], WORDS, GROUPED + 13.5) + (0,)
         multiply(1, 1)
-        copy_first(0)
-        last = placed("last", [P, PACK, CHUNK], BF16, GROUPED + 10)
-        for t in range(PACK):
-            gather(3, t)
-        copy_first(1)
-        rectify(2)
-        quantize_chunk(2)
-        multiply(2, 0)
-        multiply(2, 1)
-        finish(0)
-        rectify(3)
-        quantize_chunk(3)
-        finish(1)
-        copy_first(2)
-        for a in range(2):
+        for c in (2, 3):
+            for t in (2, 3):
+                gather(planes_of(c)[:, t, :], t, CHUNK_START[c], CHUNK)
+        for c in (0, 1):
             for u in range(2):
-                perf(3, a, u)
+                copy_out(c, u)
+        for c in (2, 3):
+            high[c] = placed(f"high{c}", [P, WORDS], BF16, GROUPED + 8 + 2 * c)
+            rectify(high[c][:], planes_of(c))
+        multiply(2, 0)
+        finish(0, 0)
+        perf(3, 0, 0)
+        z[2, 1] = quantize("z_high2", high[2][:], WORDS) + (0,)
+        multiply(2, 1)
+        finish(0, 1, in_late(1))
+        perf(3, 0, 1)
+        finish(1, 0, kb=GROUPED + 12)
+        brand(3, 0, 0)
+        z[3, 1] = quantize("z_high3", high[3][:], WORDS) + (0,)
+        finish(1, 1, kb=GROUPED + 14)
         for u in range(2):
-            for a in range(2):
-                brand(3, a, u)
-        finish(2)
-        copy_first(3)
-        finish(3)
+            copy_out(2, u)
+        for u in range(2):
+            perf(3, 1, u)
+        brand(3, 1, 0)
+        brand(3, 0, 1)
+        brand(3, 1, 1)
+        for u in range(2):
+            copy_out(3, u)
+        for c in (2, 3):
+            for u in range(2):
+                finish(c, u)

@@ -93,7 +93,7 @@ def tile_list_slot_bidding_kernel(
         tab = [placed(f"tab{a}", [P, T], I32, TAB + 16 * a) for a in range(2)]
         tab_sc = placed("tab_sc", [P, T], U8, TAB_SC)
         picked_sc = own("picked_sc", [P, S], U8)
-        v_sc = own("v_sc", [P, 2, S], U8)
+        v_sc = [own(f"v_sc{half}", [P, 2, BANK], U8) for half in range(2)]
         wb_codes = own("wb_codes", [P, 2, 2 * N], U8)
         wb_sc = own("wb_sc", [P, 2, N], U8)
         wgs_rows = own("wgs_rows", [P, S], F32)
@@ -102,7 +102,8 @@ def tile_list_slot_bidding_kernel(
             nc.sync.dma_start(out=tab_sc[a:32:2, :].bitcast(I32), in_=tab_scales[a].bitcast(I32))
         nc.vector.memset(tab_sc[32:64, :].bitcast(I32), 0)
         nc.vector.memset(tab_sc[64:128, :].bitcast(I32), 0)
-        nc.vector.memset(v_sc[:].rearrange("p a c -> p (a c)").bitcast(I32), 0)
+        for half in range(2):
+            nc.vector.memset(v_sc[half][:].rearrange("p a c -> p (a c)").bitcast(I32), 0)
         nc.vector.memset(wb_sc[:].rearrange("p a c -> p (a c)").bitcast(I32), 0)
         nc.sync.dma_start(list1[:], offs)
         nc.sync.dma_start(out=tab[0][:], in_=tab_words[0].rearrange("p t i -> p (t i)").bitcast(I32))
@@ -113,10 +114,13 @@ def tile_list_slot_bidding_kernel(
         load_page(0)
         nc.sync.dma_start(out=wgs_rows[:, CHUNK:BANK], in_=wgs[:, CHUNK:BANK])
         nc.vector.tensor_copy(picked_sc[:], tab_sc[:].indirect(list1[:]))
-        for q in range(QUADS):
-            nc.scalar.dma_start(
-                out=v_sc[32 * q : 32 * q + 4, :, :].bitcast(I32), in_=picked_sc[8 * q : 8 * q + 8, :].bitcast(I32)
-            )
+        for half, queue in enumerate((nc.scalar, nc.sync)):
+            cols = slice(half * BANK, (half + 1) * BANK)
+            for q in range(QUADS):
+                queue.dma_start(
+                    out=v_sc[half][32 * q : 32 * q + 4, :, :].bitcast(I32),
+                    in_=picked_sc[8 * q : 8 * q + 8, cols].bitcast(I32),
+                )
         w1_b = [load("w1_b0", pass_rows(w1, 0)[:, :, P : 2 * P], W1_RAW + 4)]
         h0_last = own("h0_last", [P, 2 * BANK - TAIL], F32)
         w1_b.append(h0_last[:, BANK - TAIL :].rearrange("p (j c) -> p j c", j=PACK))
@@ -177,7 +181,7 @@ def tile_list_slot_bidding_kernel(
                     lhsT=w1_q[index, a][0].bitcast(FP8X4),
                     lhsT_scale=w1_q[index, a][1],
                     rhs=v_codes[a][:, cols].bitcast(FP8X4),
-                    rhs_scale=v_sc[:, a, cols],
+                    rhs_scale=v_sc[cols.start // BANK][:, a, cols.start % BANK : (cols.stop - 1) % BANK + 1],
                     start=(a == 0),
                     stop=(a == 1),
                 )

@@ -116,19 +116,20 @@ def tile_list_slot_bidding_kernel(
         nc.vector.tensor_copy(picked_sc[:], tab_sc[:].indirect(list1[:]))
         for half, queue in enumerate((nc.scalar, nc.sync)):
             cols = slice(half * BANK, (half + 1) * BANK)
-            for q in range(QUADS):
+            for q in (0, 2, 1, 3):
                 queue.dma_start(
                     out=v_sc[half][32 * q : 32 * q + 4, :, :].bitcast(I32),
                     in_=picked_sc[8 * q : 8 * q + 8, cols].bitcast(I32),
                 )
-        w1_b = [load("w1_b0", pass_rows(w1, 0)[:, :, P : 2 * P], W1_RAW + 4)]
         h0_last = own("h0_last", [P, 2 * BANK - TAIL], F32)
-        w1_b.append(h0_last[:, BANK - TAIL :].rearrange("p (j c) -> p j c", j=PACK))
-        nc.sync.dma_start(out=w1_b[1], in_=pass_rows(w1, 1)[:, :, P : 2 * P])
+        w1_b = [h0_last[:, BANK - TAIL :].rearrange("p (j c) -> p j c", j=PACK)]
+        nc.sync.dma_start(out=w1_b[0], in_=pass_rows(w1, 0)[:, :, P : 2 * P])
         nc.sync.dma_start(out=wgs_rows[:, BANK:], in_=wgs[:, BANK:])
+        w1_b.append(load("w1_b1", pass_rows(w1, 1)[:, :, P : 2 * P], W1_RAW + 4))
         nc.sync.dma_start(list3[:], offs3)
+        w1_c = [load("w1_c0", pass_rows(w1, 0)[:, :, 2 * P : K_PASS], W1_RAW + 8)]
         load_page(1)
-        w1_c = load_w1("w1_c", 2 * P, K_PASS)
+        w1_c.append(load("w1_c1", pass_rows(w1, 1)[:, :, 2 * P : K_PASS], W1_RAW + 12))
         load_page(2)
         load_page(3)
         w1_d = load_w1("w1_d", K_PASS, H)
@@ -156,6 +157,14 @@ def tile_list_slot_bidding_kernel(
                     cols = slice(a * width + b * P, a * width + (b + 1) * P)
                     w1_q[first_tile + b, a] = (codes[:, cols], scales[:, cols])
 
+        def quantize_w1_pass(name, raw, a, first_tile, count):
+            width = count * P
+            grouped = placed(f"g_{name}{a}", [P, PACK * width], BF16, GROUPED + 2 * first_tile + a * count)
+            nc.scalar.copy(out=woven(grouped[:]), in_=planar(raw[a][:]))
+            codes, scales = quantize(f"{name}{a}", grouped[:], PACK * width)
+            for b in range(count):
+                w1_q[first_tile + b, a] = (codes[:, b * P : (b + 1) * P], scales[:, b * P : (b + 1) * P])
+
         quantize_w1("w1_a", w1_a, 0, 1)
 
         v_codes.append(placed("v_codes1", [P, S], U32, TAB_SC))
@@ -174,50 +183,73 @@ def tile_list_slot_bidding_kernel(
                 in_=wb_scales[:, 4 * q : 4 * q + 4, :].rearrange("a r c -> r a c").bitcast(I32),
             )
 
-        def h_part(index, cols, bank, dest, split=None):
-            for a in range(2):
-                nc.tensor.matmul_mx(
-                    out=bank,
-                    lhsT=w1_q[index, a][0].bitcast(FP8X4),
-                    lhsT_scale=w1_q[index, a][1],
-                    rhs=v_codes[a][:, cols].bitcast(FP8X4),
-                    rhs_scale=v_sc[cols.start // BANK][:, a, cols.start % BANK : (cols.stop - 1) % BANK + 1],
-                    start=(a == 0),
-                    stop=(a == 1),
-                )
-            if split is None:
-                nc.scalar.copy(out=dest, in_=bank)
-            else:
-                nc.scalar.copy(out=dest[:, :split], in_=bank[:, :split])
-                nc.scalar.copy(out=dest[:, split:], in_=bank[:, split:])
+        def h_pass(index, a, cols, bank):
+            nc.tensor.matmul_mx(
+                out=bank,
+                lhsT=w1_q[index, a][0].bitcast(FP8X4),
+                lhsT_scale=w1_q[index, a][1],
+                rhs=v_codes[a][:, cols].bitcast(FP8X4),
+                rhs_scale=v_sc[cols.start // BANK][:, a, cols.start % BANK : (cols.stop - 1) % BANK + 1],
+                start=(a == 0),
+                stop=(a == 1),
+            )
+
+        halves = [slice(u * BANK, (u + 1) * BANK) for u in range(2)]
+
+        def open_h(index, first_bank):
+            for u in range(2):
+                h_pass(index, 0, halves[u], banks[first_bank + u][:])
+
+        def close_h(index, first_bank, dest):
+            for u in range(2):
+                h_pass(index, 1, halves[u], banks[first_bank + u][:])
+                if dest is not None:
+                    nc.scalar.copy(out=dest[:, halves[u]], in_=banks[first_bank + u][:])
 
         def make_h(index, dest, first_bank):
             for u in range(2):
-                cols = slice(u * BANK, (u + 1) * BANK)
-                h_part(index, cols, banks[first_bank + u][:], dest[:, cols])
+                for a in range(2):
+                    h_pass(index, a, halves[u], banks[first_bank + u][:])
+                nc.scalar.copy(out=dest[:, halves[u]], in_=banks[first_bank + u][:])
 
         hs = {}
 
+        def h_tile(index):
+            hs[index] = placed(f"h{index}", [P, S], F32, W1_RAW + 8 if index == 1 else H_TILES + 4 * index)
+            return hs[index]
+
         def make_h_tile(index):
-            hs[index] = placed(f"h{index}", [P, S], F32, H_TILES + 4 * index)
-            make_h(index, hs[index], 2 * index % 8)
+            make_h(index, h_tile(index), 2 * index % 8)
 
         for n, (first, last) in enumerate(pieces):
+            bank = banks[(0, 1, 7)[n]][:, : last - first]
             if n == 2:
-                quantize_w1("w1_b", w1_b, 1, 1)
+                quantize_w1_pass("w1_b", w1_b, 0, 1, 1)
+            for a in range(2):
+                h_pass(0, a, slice(first, last), bank)
+            if n == 2:
                 part = h0_last[:, :BANK]
-                h_part(0, slice(first, last), banks[7][:], part, BANK - TAIL)
+                nc.scalar.copy(out=part[:, : BANK - TAIL], in_=bank[:, : BANK - TAIL])
+                nc.scalar.copy(out=part[:, BANK - TAIL :], in_=bank[:, BANK - TAIL :])
             else:
                 part = placed(f"h0_{n}", [P, last - first], F32, H_TILES + n)[:]
-                h_part(0, slice(first, last), banks[n][:, : last - first], part)
+                nc.scalar.copy(out=part, in_=bank)
             nc.vector.tensor_tensor(
                 pages[0][:].indirect(entries(list2, first, last - first)), part, wgs_rows[:, first:last], MULT
             )
 
-        make_h_tile(1)
-        quantize_w1("w1_c", w1_c, 2, 2)
-        make_h_tile(2)
-        make_h_tile(3)
+        open_h(1, 2)
+        quantize_w1_pass("w1_b", w1_b, 1, 1, 1)
+        close_h(1, 2, None)
+        quantize_w1_pass("w1_c", w1_c, 0, 2, 2)
+        h_tile(1)
+        for u in range(2):
+            nc.scalar.copy(out=hs[1][:, halves[u]], in_=banks[2 + u][:])
+        for index in (2, 3):
+            open_h(index, 2 * index)
+        quantize_w1_pass("w1_c", w1_c, 1, 2, 2)
+        for index in (2, 3):
+            close_h(index, 2 * index, h_tile(index))
 
         grouped = placed("g_w1_d", [P, 2 * PACK * K_PASS], BF16, GROUPED + 8)
         for a in range(2):
@@ -239,7 +271,7 @@ def tile_list_slot_bidding_kernel(
         for index in range(4):
             if index > 0:
                 nc.vector.tensor_tensor(pages[index][:].indirect(list2[:]), hs[index][:], wgs_rows[:], MULT)
-            x_rows = placed(f"x_rows{index}", [P, SLOTS], BF16, W1_RAW + (12, 14, 24, 26)[index])
+            x_rows = placed(f"x_rows{index}", [P, SLOTS], BF16, W1_RAW + (4, 12, 24, 26)[index])
             nc.vector.tensor_copy(x_rows[:], pages[index][:].indirect(list3[:]))
             nc.sync.dma_start(out=x_planes[32 * index : 32 * index + 32, :, :], in_=x_rows[:])
         load_page(7)

@@ -109,10 +109,9 @@ def tile_list_slot_bidding_kernel(
         nc.sync.dma_start(out=tab[0][:], in_=tab_words[0].rearrange("p t i -> p (t i)").bitcast(I32))
         w1_a = load_w1("w1_a", 0, P, nc.scalar)
         nc.sync.dma_start(out=tab[1][:], in_=tab_words[1].rearrange("p t i -> p (t i)").bitcast(I32))
-        nc.sync.dma_start(out=wgs_rows[:, 0:CHUNK], in_=wgs[:, 0:CHUNK])
+        nc.sync.dma_start(out=wgs_rows[:, :BANK], in_=wgs[:, :BANK])
         nc.sync.dma_start(list2[:], offs2)
         load_page(0)
-        nc.sync.dma_start(out=wgs_rows[:, CHUNK:BANK], in_=wgs[:, CHUNK:BANK])
         nc.vector.tensor_copy(picked_sc[:], tab_sc[:].indirect(list1[:]))
         for half, queue in enumerate((nc.scalar, nc.sync)):
             cols = slice(half * BANK, (half + 1) * BANK)
@@ -221,22 +220,21 @@ def tile_list_slot_bidding_kernel(
         def make_h_tile(index):
             make_h(index, h_tile(index), 2 * index % 8)
 
-        for n, (first, last) in enumerate(pieces):
-            bank = banks[(0, 1, 7)[n]][:, : last - first]
-            if n == 2:
-                quantize_w1_pass("w1_b", w1_b, 0, 1, 1)
+        h0_first = placed("h0_first", [P, BANK], F32, H_TILES)
+        for n in range(2):
+            cols = slice(n * CHUNK, (n + 1) * CHUNK)
             for a in range(2):
-                h_pass(0, a, slice(first, last), bank)
-            if n == 2:
-                part = h0_last[:, :BANK]
-                nc.scalar.copy(out=part[:, : BANK - TAIL], in_=bank[:, : BANK - TAIL])
-                nc.scalar.copy(out=part[:, BANK - TAIL :], in_=bank[:, BANK - TAIL :])
-            else:
-                part = placed(f"h0_{n}", [P, last - first], F32, H_TILES + n)[:]
-                nc.scalar.copy(out=part, in_=bank)
-            nc.vector.tensor_tensor(
-                pages[0][:].indirect(entries(list2, first, last - first)), part, wgs_rows[:, first:last], MULT
-            )
+                h_pass(0, a, cols, banks[n][:, :CHUNK])
+            nc.scalar.copy(out=h0_first[:, cols], in_=banks[n][:, :CHUNK])
+        nc.vector.tensor_tensor(pages[0][:].indirect(entries(list2, 0, BANK)), h0_first[:], wgs_rows[:, :BANK], MULT)
+        quantize_w1_pass("w1_b", w1_b, 0, 1, 1)
+        for a in range(2):
+            h_pass(0, a, halves[1], banks[7][:])
+        nc.scalar.copy(out=h0_last[:, : BANK - TAIL], in_=banks[7][:, : BANK - TAIL])
+        nc.scalar.copy(out=h0_last[:, BANK - TAIL : BANK], in_=banks[7][:, BANK - TAIL :])
+        nc.vector.tensor_tensor(
+            pages[0][:].indirect(entries(list2, BANK, BANK)), h0_last[:, :BANK], wgs_rows[:, BANK:], MULT
+        )
 
         open_h(1, 2)
         quantize_w1_pass("w1_b", w1_b, 1, 1, 1)

@@ -113,10 +113,10 @@ def tile_list_slot_bidding_kernel(
         nc.sync.dma_start(list2[:], offs2)
         load_page(0)
         nc.vector.tensor_copy(picked_sc[:], tab_sc[:].indirect(list1[:]))
-        for half, queue in enumerate((nc.scalar, nc.sync)):
+        for half, queues in enumerate(((nc.scalar, nc.gpsimd), (nc.sync, nc.sync))):
             cols = slice(half * BANK, (half + 1) * BANK)
             for q in (0, 2, 1, 3):
-                queue.dma_start(
+                queues[q % 2].dma_start(
                     out=v_sc[half][32 * q : 32 * q + 4, :, :].bitcast(I32),
                     in_=picked_sc[8 * q : 8 * q + 8, cols].bitcast(I32),
                 )

@@ -427,6 +427,10 @@ def tile_list_slot_bidding_kernel(
         brand(3, 1, 1)
         for u in range(2):
             copy_out(3, u)
-        for c in (2, 3):
-            for u in range(2):
-                finish(c, u)
+        for c, u in ((2, 0), (2, 1), (3, 0)):
+            finish(c, u)
+        last = placed("result3_1", [P, BANK], F32, W1_RAW + 30)
+        for e in range(2):
+            cols = slice(e * CHUNK, (e + 1) * CHUNK)
+            nc.vector.tensor_tensor(last[:, cols], banks[brand_banks[3][1]][:, cols], copied[3, 1][:, cols], MAX)
+            nc.sync.dma_start(out=out_view[:, 2 + e, CHUNK_START[3] :], in_=last[:, cols])

from contextlib import ExitStack

import concourse.mybir as mybir

K, T, S, H, T2, SLOTS, N = 1024, 4096, 1024, 1024, 2048, 1024, 512
FLOPS = 2 * K * H * S + 2 * 2 * H * N * SLOTS

F32 = mybir.dt.float32
BF16 = mybir.dt.bfloat16
I32 = mybir.dt.int32
U32 = mybir.dt.uint32
U16 = mybir.dt.uint16
U8 = mybir.dt.uint8
FP8X4 = mybir.dt.float8_e4m3fn_x4
FP4X4 = mybir.dt.float4_e2m1fn_x4
MULT = mybir.AluOpType.mult
MAX = mybir.AluOpType.max
RELU = mybir.ActivationFunctionType.Relu

P = 128
PACK = 4
K_PASS = P * PACK
BANK = 512
CHUNK = 256
QUADS = 4
TAIL = 64
KB = 1024

TAB, TAB_SC, PAGES, W1_RAW, PLANES, H_TILES, GROUPED, X_PLANES = 0, 32, 36, 84, 116, 132, 164, 180

CHUNK_START = (0, CHUNK, 2 * CHUNK, 3 * CHUNK)


def tile_list_slot_bidding_kernel(
    tc, tab_words, tab_scales, offs, offs2, offs3, w1, wgs, page0, wb_words, wb_scales, wp, out
):
    nc = tc.nc
    with ExitStack() as ctx:
        lists = ctx.enter_context(tc.tile_pool(name="lists", bufs=1))
        keep = ctx.enter_context(tc.tile_pool(name="keep", bufs=1))
        shared = ctx.enter_context(tc.tile_pool(name="shared", bufs=1))
        psum = ctx.enter_context(tc.psum_pool(name="psum", bufs=1))
        banks = [psum.tile([P, BANK], F32, name=f"bank{b}") for b in range(8)]

        def own(name, shape, dtype):
            return keep.tile(shape, dtype, name=name, align_bytes=64)

        def placed(name, shape, dtype, kb):
            return shared.tile(shape, dtype, name=name, align_bytes=64, offset=int(kb * KB))

        def entries(index_list, first, count):
            return index_list[:, first // 16 : (first + count) // 16]

        def pass_rows(w, a):
            return w[a * K_PASS : (a + 1) * K_PASS, :].rearrange("(p j) c -> p j c", j=PACK)

        def woven(flat):
            return flat.rearrange("p (c i j) -> p c j i", i=4, j=PACK)

        def planar(planes):
            return planes.rearrange("p j (c i) -> p c j i", i=4)

        def load(name, rows, kb, queue=nc.sync):
            raw = placed(name, list(rows.shape), F32, kb)
            queue.dma_start(out=raw[:], in_=rows)
            return raw

        def load_w1(name, first, last, queue=nc.sync):
            kb = W1_RAW + first // 32
            width_kb = (last - first) // 64
            return [load(f"{name}{a}", pass_rows(w1, a)[:, :, first:last], kb + width_kb * a, queue) for a in range(2)]

        pages = {}

        def load_page(index):
            kb = PAGES + 8 * index if index < 6 else TAB + 16 + 8 * (index - 6)
            if index < 4:
                rows = page0[index * P : (index + 1) * P, :]
            else:
                rows = page0[K_PASS:, :].rearrange("(p i) t -> i p t", i=PACK)[index - 4]
            pages[index] = load(f"page{index}", rows, kb)

        def quantize(name, grouped, width, kb=None):
            shape = [P, width // PACK]
            codes = own(name + "_codes", shape, U32) if kb is None else placed(name + "_codes", shape, U32, kb)
            scales = own(name + "_sc", shape, U8)
            nc.vector.quantize_mx(out=codes[:].bitcast(FP8X4), scales=scales[:], in_=grouped)
            return codes, scales

        list1 = lists.tile([P, S // 16], U16, name="list1")
        list2 = lists.tile([P, S // 16], U16, name="list2")
        list3 = lists.tile([P, SLOTS // 16], U16, name="list3")
        tab = [placed(f"tab{a}", [P, T], I32, TAB + 16 * a) for a in range(2)]
        tab_sc = placed("tab_sc", [P, T], U8, TAB_SC)
        picked_sc = own("picked_sc", [P, S], U8)
        v_sc = [own(f"v_sc{half}", [P, 2, BANK], U8) for half in range(2)]
        wb_codes = own("wb_codes", [P, 2, 2 * N], U8)
        wb_sc = own("wb_sc", [P, 2, N], U8)
        wgs_rows = own("wgs_rows", [P, S], F32)

        for a in range(2):
            nc.sync.dma_start(out=tab_sc[a:32:2, :].bitcast(I32), in_=tab_scales[a].bitcast(I32))
        nc.vector.memset(tab_sc[32:64, :].bitcast(I32), 0)
        nc.vector.memset(tab_sc[64:128, :].bitcast(I32), 0)
        for half in range(2):
            nc.vector.memset(v_sc[half][:].rearrange("p a c -> p (a c)").bitcast(I32), 0)
        nc.vector.memset(wb_sc[:].rearrange("p a c -> p (a c)").bitcast(I32), 0)
        nc.sync.dma_start(list1[:], offs)
        nc.sync.dma_start(out=tab[0][:], in_=tab_words[0].rearrange("p t i -> p (t i)").bitcast(I32))
        w1_a = load_w1("w1_a", 0, P, nc.scalar)
        nc.sync.dma_start(out=tab[1][:], in_=tab_words[1].rearrange("p t i -> p (t i)").bitcast(I32))
        nc.sync.dma_start(out=wgs_rows[:, :BANK], in_=wgs[:, :BANK])
        nc.sync.dma_start(list2[:], offs2)
        load_page(0)
        nc.vector.tensor_copy(picked_sc[:], tab_sc[:].indirect(list1[:]))
        for half, queues in enumerate(((nc.scalar, nc.gpsimd), (nc.sync, nc.sync))):
            cols = slice(half * BANK, (half + 1) * BANK)
            for q in (0, 2, 1, 3):
                queues[q % 2].dma_start(
                    out=v_sc[half][32 * q : 32 * q + 4, :, :].bitcast(I32),
                    in_=picked_sc[8 * q : 8 * q + 8, cols].bitcast(I32),
                )
        h0_last = own("h0_last", [P, 2 * BANK - TAIL], F32)
        w1_b = [h0_last[:, BANK - TAIL :].rearrange("p (j c) -> p j c", j=PACK)]
        nc.sync.dma_start(out=w1_b[0], in_=pass_rows(w1, 0)[:, :, P : 2 * P])
        nc.sync.dma_start(out=wgs_rows[:, BANK:], in_=wgs[:, BANK:])
        w1_b.append(load("w1_b1", pass_rows(w1, 1)[:, :, P : 2 * P], W1_RAW + 4))
        nc.sync.dma_start(list3[:], offs3)
        w1_c = [load("w1_c0", pass_rows(w1, 0)[:, :, 2 * P : K_PASS], W1_RAW + 8)]
        load_page(1)
        w1_c.append(load("w1_c1", pass_rows(w1, 1)[:, :, 2 * P : K_PASS], W1_RAW + 12))
        load_page(2)
        load_page(3)
        w1_d = load_w1("w1_d", K_PASS, H)
        wgs_planes = placed("wgs_planes", [P, PACK, S], F32, PLANES)
        for q in (0, 2, 1, 3):
            nc.sync.dma_start(
                out=wgs_planes[32 * q : 32 * q + 32, :, :], in_=wgs.rearrange("(q i) j -> q i j", i=PACK)
            )
        load_page(4)
        load_page(5)

        v_codes = [own("v_codes0", [P, S], U32)]
        nc.vector.tensor_copy(v_codes[0][:], tab[0][:].bitcast(U32).indirect(list1[:]))

        w1_q = {}

        def quantize_w1(name, raw, first_tile, count):
            width = count * P
            grouped = placed("g_" + name, [P, 2 * PACK * width], BF16, GROUPED + 2 * first_tile)
            for a in range(2):
                nc.scalar.copy(out=woven(grouped[:, a * PACK * width : (a + 1) * PACK * width]), in_=planar(raw[a][:]))
            codes, scales = quantize(name, grouped[:], 2 * PACK * width)
            for b in range(count):
                for a in range(2):
                    cols = slice(a * width + b * P, a * width + (b + 1) * P)
                    w1_q[first_tile + b, a] = (codes[:, cols], scales[:, cols])

        def quantize_w1_pass(name, raw, a, first_tile, count):
            width = count * P
            grouped = placed(f"g_{name}{a}", [P, PACK * width], BF16, GROUPED + 2 * first_tile + a * count)
            nc.scalar.copy(out=woven(grouped[:]), in_=planar(raw[a][:]))
            codes, scales = quantize(f"{name}{a}", grouped[:], PACK * width)
            for b in range(count):
                w1_q[first_tile + b, a] = (codes[:, b * P : (b + 1) * P], scales[:, b * P : (b + 1) * P])

        quantize_w1("w1_a", w1_a, 0, 1)

        v_codes.append(placed("v_codes1", [P, S], U32, TAB_SC))
        pieces = ((0, CHUNK), (CHUNK, BANK), (BANK, S))
        for first, last in pieces:
            nc.vector.tensor_copy(
                v_codes[1][:, first:last], tab[1][:].bitcast(U32).indirect(entries(list1, first, last - first))
            )

        load_page(6)
        wp_raw = [load(f"wp_raw{a}", pass_rows(wp, a), TAB + 8 * a) for a in range(2)]
        nc.sync.dma_start(out=wb_codes[:].bitcast(I32), in_=wb_words.rearrange("a p c -> p a c").bitcast(I32))
        for q in range(QUADS):
            nc.sync.dma_start(
                out=wb_sc[32 * q : 32 * q + 4, :, :].bitcast(I32),
                in_=wb_scales[:, 4 * q : 4 * q + 4, :].rearrange("a r c -> r a c").bitcast(I32),
            )

        def h_pass(index, a, cols, bank):
            nc.tensor.matmul_mx(
                out=bank,
                lhsT=w1_q[index, a][0].bitcast(FP8X4),
                lhsT_scale=w1_q[index, a][1],
                rhs=v_codes[a][:, cols].bitcast(FP8X4),
                rhs_scale=v_sc[cols.start // BANK][:, a, cols.start % BANK : (cols.stop - 1) % BANK + 1],
                start=(a == 0),
                stop=(a == 1),
            )

        halves = [slice(u * BANK, (u + 1) * BANK) for u in range(2)]

        def open_h(index, first_bank):
            for u in range(2):
                h_pass(index, 0, halves[u], banks[first_bank + u][:])

        def close_h(index, first_bank, dest):
            for u in range(2):
                h_pass(index, 1, halves[u], banks[first_bank + u][:])
                if dest is not None:
                    nc.scalar.copy(out=dest[:, halves[u]], in_=banks[first_bank + u][:])

        def make_h(index, dest, first_bank):
            for u in range(2):
                for a in range(2):
                    h_pass(index, a, halves[u], banks[first_bank + u][:])
                nc.scalar.copy(out=dest[:, halves[u]], in_=banks[first_bank + u][:])

        hs = {}

        def h_tile(index):
            hs[index] = placed(f"h{index}", [P, S], F32, W1_RAW + 8 if index == 1 else H_TILES + 4 * index)
            return hs[index]

        def make_h_tile(index):
            make_h(index, h_tile(index), 2 * index % 8)

        h0_first = placed("h0_first", [P, BANK], F32, H_TILES)
        for n in range(2):
            cols = slice(n * CHUNK, (n + 1) * CHUNK)
            for a in range(2):
                h_pass(0, a, cols, banks[n][:, :CHUNK])
            nc.scalar.copy(out=h0_first[:, cols], in_=banks[n][:, :CHUNK])
        nc.vector.tensor_tensor(pages[0][:].indirect(entries(list2, 0, BANK)), h0_first[:], wgs_rows[:, :BANK], MULT)
        quantize_w1_pass("w1_b", w1_b, 0, 1, 1)
        for a in range(2):
            h_pass(0, a, halves[1], banks[7][:])
        nc.scalar.copy(out=h0_last[:, : BANK - TAIL], in_=banks[7][:, : BANK - TAIL])
        nc.scalar.copy(out=h0_last[:, BANK - TAIL : BANK], in_=banks[7][:, BANK - TAIL :])
        nc.vector.tensor_tensor(
            pages[0][:].indirect(entries(list2, BANK, BANK)), h0_last[:, :BANK], wgs_rows[:, BANK:], MULT
        )

        open_h(1, 2)
        quantize_w1_pass("w1_b", w1_b, 1, 1, 1)
        close_h(1, 2, None)
        quantize_w1_pass("w1_c", w1_c, 0, 2, 2)
        h_tile(1)
        for u in range(2):
            nc.scalar.copy(out=hs[1][:, halves[u]], in_=banks[2 + u][:])
        for index in (2, 3):
            open_h(index, 2 * index)
        quantize_w1_pass("w1_c", w1_c, 1, 2, 2)
        for index in (2, 3):
            close_h(index, 2 * index, h_tile(index))

        grouped = placed("g_w1_d", [P, 2 * PACK * K_PASS], BF16, GROUPED + 8)
        for a in range(2):
            nc.scalar.copy(
                out=grouped[:, a * PACK * K_PASS : (a + 1) * PACK * K_PASS].rearrange(
                    "p (t m j) -> p m j t", t=PACK, j=PACK
                ),
                in_=w1_d[a][:].rearrange("p j (m t) -> p m j t", t=PACK),
            )
        codes, scales = quantize("w1_d", grouped[:], 2 * PACK * K_PASS)
        for a in range(2):
            for t in range(PACK):
                cols = slice(a * K_PASS + t * P, a * K_PASS + (t + 1) * P)
                w1_q[4 + t, a] = (codes[:, cols], scales[:, cols])
        for index in range(4, 7):
            make_h_tile(index)

        x_planes = placed("x_planes", [P, PACK, SLOTS], BF16, X_PLANES)
        for index in range(4):
            if index > 0:
                nc.vector.tensor_tensor(pages[index][:].indirect(list2[:]), hs[index][:], wgs_rows[:], MULT)
            x_rows = placed(f"x_rows{index}", [P, SLOTS], BF16, W1_RAW + (4, 12, 24, 26)[index])
            nc.vector.tensor_copy(x_rows[:], pages[index][:].indirect(list3[:]))
            nc.sync.dma_start(out=x_planes[32 * index : 32 * index + 32, :, :], in_=x_rows[:])
        load_page(7)

        def scatter(t, h):
            nc.vector.tensor_tensor(pages[4 + t][:].indirect(list2[:]), h, wgs_planes[:, t, :], MULT)

        for t in range(3):
            scatter(t, hs[4 + t][:])

        wp_grouped = placed("g_wp", [P, 2 * PACK * N], BF16, GROUPED)
        for a in range(2):
            nc.scalar.copy(out=woven(wp_grouped[:, a * PACK * N : (a + 1) * PACK * N]), in_=planar(wp_raw[a][:]))
        wp_codes, wp_sc = quantize("wp", wp_grouped[:], 2 * PACK * N)

        WORDS = PACK * CHUNK

        def rectify(dest, planes):
            nc.scalar.activation(woven(dest), planar(planes), RELU)

        low_0 = placed("low_0", [P, WORDS], BF16, TAB)
        low_12 = placed("low_12", [P, 2 * WORDS], BF16, TAB + 2)
        high0_low3 = placed("high0_low3", [P, 2 * WORDS], BF16, TAB + 8)
        rectify(low_12[:], x_planes[:, :, CHUNK : 3 * CHUNK])
        rectify(high0_low3[:, WORDS:], x_planes[:, :, 3 * CHUNK :])
        rectify(low_0[:], x_planes[:, :, :CHUNK])
        z = {(0, 0): quantize("z_low0", low_0[:], WORDS, H_TILES + 28) + (0,)}

        late = placed("late", [P, 25 * CHUNK], BF16, X_PLANES)

        def runs(first, pitch, count, width):
            lead = min(first, pitch - width)
            start = int((first - lead) * CHUNK)
            whole = late[:, start : start + int(count * pitch * CHUNK)].rearrange("p (r s) -> p r s", r=count)
            return whole[:, :, int(lead * CHUNK) : int((lead + width) * CHUNK)]

        h7 = runs(0, 8, 1, 8)[:, 0, :].bitcast(F32)
        make_h(7, h7, 2)
        plane_places = ((8, 1), (12.5, 3.75), (4, 4), (5, 6))

        def planes_of(c):
            return runs(plane_places[c][0], plane_places[c][1], PACK, 1)

        def plane_pair(c0, c1, t):
            first, second = (plane_places[c][0] + t * plane_places[c][1] for c in (c0, c1))
            return runs(first, second - first, 2, 1)

        out_view = out.rearrange("(b p) m -> p b m", p=P)
        brand_banks = ((0, 1), (4, 5), (0, 1), (6, 0))
        perf_banks = ((2, 3), (6, 7), (4, 5), (2, 3))

        def passes(c, a, u, bank, weights):
            codes, scales, base = z[c, a]
            cols = slice(base, base + CHUNK)
            for e in range(2):
                w_codes, w_scales = weights(a, 2 * u + e)
                nc.tensor.matmul_mx(
                    out=banks[bank][:, e * CHUNK : (e + 1) * CHUNK],
                    lhsT=w_codes,
                    lhsT_scale=w_scales,
                    rhs=codes[:, cols].bitcast(FP8X4),
                    rhs_scale=scales[:, cols],
                    start=(a == 0 and e == 0),
                    stop=(a == 1 and e == 1),
                )

        def brand_weights(a, b):
            return wb_codes[:, a, 2 * b * P : 2 * (b + 1) * P].bitcast(FP4X4), wb_sc[:, a, b * P : (b + 1) * P]

        def perf_weights(a, b):
            cols = slice(a * N + b * P, a * N + (b + 1) * P)
            return wp_codes[:, cols].bitcast(FP8X4), wp_sc[:, cols]

        def brand(c, a, u):
            passes(c, a, u, brand_banks[c][u], brand_weights)

        def perf(c, a, u):
            passes(c, a, u, perf_banks[c][u], perf_weights)

        def multiply(c, a):
            for product in (brand, perf):
                for u in range(2):
                    product(c, a, u)

        def gather(dest, t, first, count):
            nc.vector.tensor_copy(dest, pages[4 + t][:].indirect(entries(list3, first, count)))

        copied = {}

        def copy_out(c, u):
            copied[c, u] = placed(f"copied{c}_{u}", [P, BANK], F32, W1_RAW + 4 * c + 2 * u)
            nc.scalar.copy(out=copied[c, u][:], in_=banks[(perf_banks if c == 3 else brand_banks)[c][u]][:])

        def finish(c, u, result=None, kb=None):
            if result is None:
                own_result = placed(f"result{c}_{u}", [P, BANK], F32, kb or W1_RAW + 16 + 4 * c + 2 * u)
                result = own_result[:].rearrange("p (e m) -> p e m", e=2)
            other = banks[(brand_banks if c == 3 else perf_banks)[c][u]]
            nc.vector.tensor_tensor(
                result,
                other[:].rearrange("p (e m) -> p e m", e=2),
                copied[c, u][:].rearrange("p (e m) -> p e m", e=2),
                MAX,
            )
            nc.sync.dma_start(out=out_view[:, 2 * u : 2 * u + 2, CHUNK_START[c] : CHUNK_START[c] + CHUNK], in_=result)

        def in_late(first):
            return runs(first, 2, 2, 2).bitcast(F32)

        multiply(0, 0)
        for t in range(3):
            gather(plane_pair(0, 1, t), t, 0, 2 * CHUNK)
        scatter(3, h7)
        middle = quantize("z_low12", low_12[:], 2 * WORDS, H_TILES + 28)
        z[1, 0], z[2, 0] = middle + (0,), middle + (CHUNK,)
        multiply(1, 0)
        for c in (0, 1):
            gather(planes_of(c)[:, 3, :], 3, CHUNK_START[c], CHUNK)
        gather(plane_pair(2, 3, 0), 0, 2 * CHUNK, 2 * CHUNK)
        rectify(high0_low3[:, :WORDS], planes_of(0))
        both = quantize("z_high0", high0_low3[:], 2 * WORDS)
        z[0, 1], z[3, 0] = both + (0,), both + (CHUNK,)
        multiply(0, 1)
        gather(plane_pair(2, 3, 1), 1, 2 * CHUNK, 2 * CHUNK)
        high = {1: placed("high1", [P, WORDS], BF16, GROUPED + 8)}
        rectify(high[1][:], planes_of(1))
        z[1, 1] = quantize("z_high1", high[1][:], WORDS, GROUPED + 13.5) + (0,)
        multiply(1, 1)
        for c in (2, 3):
            for t in (2, 3):
                gather(planes_of(c)[:, t, :], t, CHUNK_START[c], CHUNK)
        for c in (0, 1):
            for u in range(2):
                copy_out(c, u)
        for c in (2, 3):
            high[c] = placed(f"high{c}", [P, WORDS], BF16, GROUPED + 8 + 2 * c)
            rectify(high[c][:], planes_of(c))
        multiply(2, 0)
        finish(0, 0)
        perf(3, 0, 0)
        z[2, 1] = quantize("z_high2", high[2][:], WORDS) + (0,)
        multiply(2, 1)
        finish(0, 1, in_late(1))
        perf(3, 0, 1)
        finish(1, 0, kb=GROUPED + 12)
        brand(3, 0, 0)
        z[3, 1] = quantize("z_high3", high[3][:], WORDS) + (0,)
        finish(1, 1, kb=GROUPED + 14)
        for u in range(2):
            copy_out(2, u)
        for u in range(2):
            perf(3, 1, u)
        brand(3, 1, 0)
        brand(3, 0, 1)
        brand(3, 1, 1)
        for u in range(2):
            copy_out(3, u)
        for c, u in ((2, 0), (2, 1), (3, 0)):
            finish(c, u)
        last = placed("result3_1", [P, BANK], F32, W1_RAW + 30)
        for e in range(2):
            cols = slice(e * CHUNK, (e + 1) * CHUNK)
            nc.vector.tensor_tensor(last[:, cols], banks[brand_banks[3][1]][:, cols], copied[3, 1][:, cols], MAX)
            nc.sync.dma_start(out=out_view[:, 2 + e, CHUNK_START[3] :], in_=last[:, cols])
